import numpy as np, ml_dtypes
CORES = [1,5,17,21,33,37,49,53]
N = 8
import mx_ref
BF = ml_dtypes.bfloat16
def gcols(t, e):
    v = np.concatenate([t.reshape(8, 16, -1, 4), np.zeros((8, 16, 1, 4), BF)], axis=2)
    return np.ascontiguousarray(np.stack([v[g][:, e[g]] for g in range(8)])).reshape(128, -1)
def tile(rs):
    return np.stack(rs, axis=2).reshape(128, -1).astype(BF)
def cut(t, i, w=512):
    return t[:, w * i:w * i + w]
def pick(q, e):
    c = np.concatenate([q[0].reshape(128, -1, 4), np.zeros((128, 1, 4), np.uint8)], axis=1); s = np.concatenate([q[1], np.ones((16, 1), np.uint8)], axis=1)
    return (np.ascontiguousarray(c[:, e].reshape(128, -1)), np.ascontiguousarray(s[:, e]))
def join(*qs):
    return (np.concatenate([q[0] for q in qs], axis=1), np.concatenate([q[1] for q in qs], axis=1))
def put(q, e, v):
    c, s = q[0].reshape(128, -1, 4).copy(), q[1].copy(); c[:, e] = v[0].reshape(128, -1, 4); s[:, e] = v[1]
    return (c.reshape(128, -1), s)
def pk(c, s):
    return (np.ascontiguousarray(c), mx_ref.live(s))
def emit(q):
    return q[0], q[1]
def packed(v, rng):
    q = [mx_ref.quantize(np.ascontiguousarray(v[r])) for r in range(N)]
    return np.stack([a for a, b in q]), np.stack([mx_ref.plane(b, rng) for a, b in q])
def values_of_codes():
    e, c = np.zeros((128, 128, 4), np.float32), np.zeros((128, 2, 4), np.uint8)
    e[np.arange(128), np.arange(128), 0] = 1
    c[:127, :, 0] = np.arange(256).reshape(2, 128).T[:127]
    return mx_ref.matmul(mx_ref.quantize(e.reshape(128, 512).astype(BF)), (c.reshape(128, 8), np.full((16, 2), 127, np.uint8))).T.reshape(-1).astype(np.float64)
CODE_VALUE, SCALE_VALUE = values_of_codes(), 2.0 ** (np.arange(256) - 127.0)
def decode(q):
    return (CODE_VALUE[q[0]].reshape(16, 8, -1, 4) * SCALE_VALUE[q[1]][:, None, :, None] + 0.0).reshape(128, -1).astype(np.float32)
def f(rng, *shape):
    return mx_ref.flush((rng.standard_normal(shape, dtype=np.float32) * np.exp2(rng.integers(-2, 3, shape[:-1] + (1,)))).astype(BF))
def wide(rng, *shape, cols=0):
    v = rng.standard_normal(shape, dtype=np.float32) * np.exp2(rng.integers(-12, 13, shape)).astype(np.float32)
    if cols: v *= np.repeat(np.exp2(rng.integers(-cols, cols + 1, shape[:-2] + (1, shape[-1] // 4))) * (rng.random(shape[:-2] + (1, shape[-1] // 4)) > 0.0625), 4, axis=-1).astype(np.float32)
    return mx_ref.flush(v.astype(BF))
C, L, M, R = 384, 160, 224, 3
STEP = [1, 2, 4]
def order(p):
    return np.argsort(-(p[::16] + np.float32(0.0)), axis=1, kind="stable")
def numbers_of(rng):
    return {"x": np.array(f(rng, N, 128, 4 * C)), "u": np.array(f(rng, N, 128, 512)), "v": np.array(f(rng, N, 128, 512))}
def weights(rng, still=[]):
    w = np.array(f(rng, N, 128, 2048)).reshape(N, 8, 16, 4, 8, 16, 4)
    for i in still:
        w[:, :, i] = 0
        w[:, :, :, :, :, i] = 0
    c, p = packed(w.reshape(N, 128, 2048), rng)
    return {"wc": c, "ws": p}
def signs(rng):
    return np.stack([rng.permutation(8) % 2 * 2.0 - 1.0 for r in range(N)])
def setup_inputs(rng):
    return {**numbers_of(rng), **weights(rng)}
def setup_inputs_ties(rng):
    d = numbers_of(rng)
    e = rng.permutation(N)
    x = d["x"].reshape(N, 8, 16, C, 4)
    for r in range(N):
        k = np.zeros(C, int) if r == e[0] else rng.permutation(C) % 3
        a = x[r][:, :8, :3].copy()
        a[:, :, 2] = 0
        x[r][:, :8] = a[:, :, k]
    x[e[1]] = 0
    u = d["u"].reshape(N, 8, 16, 8, 16, 4)
    k = u.copy()
    u[:, :, :, :, :2] = 0
    for g in range(8): u[:, g, :8, g, :2] = k[:, g, :8, g, :2]
    return {"x": x.reshape(N, 128, 4 * C), "u": u.reshape(N, 128, 512), "v": d["v"], **weights(rng, range(8))}
def setup_inputs_near(rng):
    d = numbers_of(rng)
    x = d["x"].astype(np.float32).reshape(N, 8, 16, C, 4)
    s = np.arange(C) // 2
    g = ((s[:, None] >> np.arange(8)) & 1) * np.exp2(np.arange(8) - 23.0)
    x[:, :, 0] = 0
    x[:, :, 0, :, 0] = signs(rng)[:, :, None]
    for r in range(N):
        for i in rng.permutation(8)[:4]: x[r, i, 0, rng.integers(C), 0] *= np.float32(2.0 ** 30)
    x[:, :, 8] = g[:, :4]
    x[:, :, 9] = g[:, 4:]
    x[:, :, 10:] = rng.integers(4, 8, (N, 8, 6, C, 4)) * rng.choice([-1.0, 1.0], (N, 8, 6, C, 4)) * 2.0 ** -20
    u = d["u"].reshape(N, 128, 128, 4)
    k = np.where(rng.permutation(N) < N // 2, 2.0 ** -30, 1.0).astype(np.float32).astype(BF)
    u[:, :, ::16] = 0
    for h in range(0, 128, 16):
        u[:, h, h, 0] = k
        u[:, h + 8:h + 10, h] = k[:, None, None]
    return {"x": x.reshape(N, 128, 4 * C).astype(BF), "u": u.reshape(N, 128, 512), "v": d["v"], **weights(rng, [0, 8, 9, 10, 11, 12, 13, 14, 15])}
def setup_inputs_starts(rng):
    d = numbers_of(rng)
    x = d["x"].astype(np.float32).reshape(N, 8, 16, C, 4)
    u = d["u"].reshape(N, 128, 128, 4)
    size = np.where(rng.permutation(N) < N // 2, 2.0 ** -30, 1.0).astype(np.float32)
    x[:, :, :11] = 0
    n = np.stack([rng.permutation([0, 1, M // 2, M - 1, M, M + 1, C - 1, C]) for r in range(N)])
    o = np.argsort(rng.random((N, 8, C)), axis=2)
    for r in range(N):
        k = rng.permutation(8)
        for g in range(8):
            x[r, g, 0, :, 0] = np.where(rng.permutation(C) < n[r, g], 1, -rng.integers(0, 2, C)) * size[r]
            if r % 2 == 0:
                a, s = o[r, g], min(int(n[r, g]), M)
                seg, rest = rng.permutation(a[s:s + L]), np.concatenate([a[:s], a[s + L:]])
                if k[g] == 0: o[r ^ 1, g] = a
                if k[g] == 1: o[r ^ 1, g] = a[::-1]
                if k[g] == 2: o[r ^ 1, g] = np.concatenate([seg, rest])
                if k[g] == 3: o[r ^ 1, g] = np.concatenate([rest, seg])
    key = C - 1 - np.argsort(o, axis=2)
    z = ((key[:, :, :, None] >> np.arange(12)) & 1) * np.exp2(np.arange(12.0))
    for i in range(3): x[:, :, 8 + i] = z[:, :, :, 4 * i:4 * i + 4]
    k = size.astype(BF)
    u[:, :, ::16] = 0
    u[:, :, 1::16] = 0
    for h in range(0, 128, 16):
        u[:, h + 8:h + 11, h] = k[:, None, None]
        u[:, h, h + 1, 0] = k
    return {"x": x.reshape(N, 128, 4 * C).astype(BF), "u": u.reshape(N, 128, 512), "v": d["v"], **weights(rng, range(11))}
def setup_inputs_huge(rng):
    d = numbers_of(rng)
    x = 2.0 ** 30 * (0.8 + 0.2 * rng.random((N, 128, C, 4)))
    c = np.ones((N, C))
    half = int(rng.integers(2))
    for r in range(N):
        if 2 * r // N == half: c[r] = rng.permutation(C) % 2 * 2.0 - 1.0
    x *= c[:, None, :, None]
    u = d["u"].reshape(N, 128, 8, 16, 4)
    a = 2.0 ** 30 * (1 - 0.1 * rng.random((N, 128, 8, 2, 4))) * np.stack([signs(rng), signs(rng)], axis=2)[:, None, :, :, None]
    u[:, :, :, :2] = a.astype(np.float32).astype(BF)
    w = np.zeros((N, 128, 4, 128, 4), np.float32)
    i = np.arange(128)
    for b in range(4): w[:, i, b, i, b] = -1
    wc, ws = packed(w.reshape(N, 128, 2048).astype(BF), rng)
    return {"x": x.astype(np.float32).reshape(N, 128, 4 * C).astype(BF), "u": u.reshape(N, 128, 512), "v": d["v"], "wc": wc, "ws": ws}
def setup_inputs_spread(rng):
    d = setup_inputs(rng)
    d["x"] = wide(rng, N, 128, 4 * C, cols=6)
    return d
def check_inputs(d):
    b = []
    for k in ("x", "u", "v"):
        a = np.abs(d[k].astype(np.float32))
        if not (np.isfinite(a).all() and ((a == 0) | (a >= 2.0 ** -30) & (a <= 2.0 ** 30)).all()): b.append("a value of " + k)
    if ((d["wc"] & 0x7F) == 0x7F).any(): b.append("a code of wc that is no number")
    z = np.zeros((128, 4, 4), np.float32)
    z[:, 1] = 2.0 ** -30
    z[:, 2] = 2.0 ** 30
    c, s = emit(mx_ref.quantize(z.reshape(128, 16).astype(BF)))
    for r in range(N):
        p = mx_ref.live(d["ws"][r])
        if not ((p == s[0, 0]) | (p >= s[0, 1]) & (p <= s[0, 2])).all(): b.append("a scale of ws")
    return b
def reference(x, u, v, wc, ws):
    qu = [mx_ref.quantize(u[r]) for r in range(N)]
    lay = [pk(wc[r], ws[r]) for r in range(N)]
    now = [x[r] for r in range(N)]
    place = np.arange(C)
    for t in range(R):
        sent, o, start = [], [], []
        for r in range(N):
            q = mx_ref.quantize(now[r])
            p = mx_ref.matmul(qu[r], q)
            sent.append(q)
            o.append(order(p))
            start.append(np.minimum(np.sum(p[1::16] > 0, axis=1), M)[:, None])
        came = decode(join(*sent)).astype(BF)
        made, child = [], []
        for r in range(N):
            e = r ^ STEP[t]
            own = (place >= start[r]) & (place < start[r] + L)
            h = o[r].copy()
            for g in range(8): h[g, ~own[g]] = o[e][g][~np.isin(o[e][g], o[r][g][own[g]])]
            c = gcols(np.concatenate([now[r], cut(came, e, 4 * C)], axis=1), np.where(own, h, C + h))
            q = mx_ref.quantize(c)
            made.append(tile([mx_ref.matmul(pick(lay[r], np.arange(128 * b, 128 * b + 128)), q) * np.float32(0.015625) + c[:, b::4].astype(np.float32) for b in range(4)]))
            child.append(h)
        now = made
    y, ot = np.zeros((N, 128, C), np.float32), np.zeros((N, 8, C), np.float32)
    oc, osc = np.zeros((N, 128, 4 * C), np.uint8), np.zeros((N, 16, C), np.uint8)
    for r in range(N):
        q = mx_ref.quantize(now[r])
        y[r] = mx_ref.matmul(mx_ref.quantize(v[r]), q)
        ot[r] = child[r]
        oc[r], osc[r] = emit(q)
    return {"y": y, "ot": ot, "oc": oc, "osc": osc}

@@ -1,0 +1,360 @@
+from concourse.mybir import dt, AluOpType as A, ActivationFunctionType as AF
+
+C, L, M, R = 384, 160, 224, 3
+STEP = [1, 2, 4]
+Q = C // 16
+NV = 14
+NS = Q - NV
+HW = 16 * (NV + 1) // 2
+PAD = HW
+BIG = 1024.0
+X4, BF, F32 = "float8_e4m3fn_x4", "bfloat16", "float32"
+
+SCRATCH = {"ps": ("psum", [128, 4096], F32)}
+for _n, _w, _d in [
+        ("ub", 512, BF), ("vb", 512, BF), ("qu", 128, X4), ("su", 128, "uint8"), ("qp", 256, X4), ("sp", 256, "uint8"),
+        ("qv", 128, X4), ("sv", 128, "uint8"), ("qw", 512, X4), ("sw", 512, "uint8"),
+        ("eb", 2048, BF), ("qe", 512, X4), ("se", 512, "uint8"),
+        ("i16", 16, "int32"), ("r16", 16, "int32"), ("ipm", Q, "int32"), ("rpm", Q, "int32"), ("pm", Q, "uint16"),
+        ("iou", 16, "int32"), ("ou", 16, "uint16"), ("iid", 128, "int32"),
+        ("dm16", 16, F32), ("kp16", 16, F32), ("t16", 16, F32), ("c16", 16, F32),
+        ("dm", C, F32), ("kp", C, BF), ("cm", C, BF), ("inv", 4, F32), ("one", C, F32), ("nb", Q, F32),
+        ("tab", C + M, BF), ("htab", 2 * C, F32),
+        ("mk", C, F32), ("hold", C, F32), ("eq", C, BF), ("cr", C, BF), ("ci", Q, F32),
+        ("fv", (NV + 1) * C, BF), ("zv", NV * C // 2, BF), ("fs", NS * C, BF),
+        ("a0", 3 * NS, F32), ("a1", PAD + 3 * NS, F32), ("ao", 3 * NS, F32),
+        ("cf", C, BF), ("cz", C // 2, BF), ("st", 4, F32), ("z16", Q, "uint16"), ("lo", Q, F32), ("hi", Q, F32),
+        ("b0", 4 * Q, F32), ("b1", 4 * Q, F32), ("bo", 4 * Q, F32),
+        ("nk", C, BF), ("val", C, F32), ("np1", C, BF), ("tc", C, BF), ("tx", C, BF), ("td", C, BF),
+        ("pl", Q, "uint16"), ("idx", C, F32), ("idd", C, F32), ("off", 5 * Q, "uint16"), ("hrow", C, F32),
+        ("ft", 4 * C, BF), ("f64", 4 * C, BF), ("t64", 4 * C, BF), ("qf", C, X4), ("sf", C, "uint8"), ("ys", C, F32)]:
+    SCRATCH[_n] = ("sbuf", [128, _w], _d)
+for _t in range(R + 1):
+    SCRATCH["win%d" % _t] = ("sbuf", [128, (8 if _t < R else 4) * C], BF)
+    SCRATCH["qt%d" % _t] = ("sbuf", [128, C], X4)
+    SCRATCH["sq%d" % _t] = ("sbuf", [128, C], "uint8")
+for _t in range(R):
+    SCRATCH["lq%d" % _t] = ("sbuf", [128, C], X4)
+    SCRATCH["ls%d" % _t] = ("sbuf", [128, C], "uint8")
+    SCRATCH["rk%d" % _t] = ("sbuf", [128, Q], "uint16")
+    SCRATCH["lr%d" % _t] = ("sbuf", [128, Q], "uint16")
+
+SEMAPHORES = ["V", "S", "P", "G", "lx", "lu", "lv", "lwc", "lws", "sent", "sty", "sto",
+              "ac0", "ac1", "ac2", "al0", "al1", "al2"]
+
+
+def schedule(g, T, ops):
+    queues = {"V": g.vector, "S": g.scalar, "P": g.tensor, "G": g, "Y": g.sync}
+    known = {q: {} for q in queues}
+    writer, readers, pos = {}, {}, {q: 0 for q in queues}
+    for n, o in enumerate(ops):
+        q = o["q"]
+        deps = set()
+        for k in o["r"]:
+            if k in writer:
+                deps.add(writer[k])
+        for k in o["w"]:
+            if k in writer:
+                deps.add(writer[k])
+            deps.update(readers.get(k, []))
+        o["waits"] = []
+        if q is not None:
+            for d in sorted(deps, reverse=True):
+                e = ops[d]
+                if e["tok"] is None or known[q].get(e["tok"], 0) >= e["at"]:
+                    continue
+                o["waits"].append(d)
+                e["inc"] = True
+                for k, v in e["clock"].items():
+                    if known[q].get(k, 0) < v:
+                        known[q][k] = v
+        if o["sem"] is not None:
+            o["tok"], o["at"] = o["sem"], 1
+        elif o["loose"]:
+            o["tok"], o["at"] = None, 0
+        else:
+            pos[q] += 1
+            o["tok"], o["at"] = q, pos[q]
+        o["clock"] = dict(known[q]) if q is not None else {}
+        if o["tok"] is not None:
+            o["clock"][o["tok"]] = o["at"]
+        for k in o["r"]:
+            readers.setdefault(k, []).append(n)
+        for k in o["w"]:
+            writer[k] = n
+            readers[k] = []
+    count = {q: 0 for q in queues}
+    for o in ops:
+        if o["q"] is None:
+            continue
+        for d in o["waits"]:
+            e = ops[d]
+            queues[o["q"]].wait_ge(T.sem[e["tok"]], e["val"])
+        ins = o["f"]()
+        if o["sem"] is not None:
+            ins.then_inc(T.sem[o["sem"]], 16)
+        elif o.get("inc"):
+            count[o["q"]] += 1
+            o["val"] = count[o["q"]]
+            ins.then_inc(T.sem[o["q"]], 1)
+
+
+def rank_program(g, core, T, topo):
+    rank = T.rank_of(core)
+    if rank is None:
+        return
+    ops = []
+    V, S = g.vector, g.scalar
+
+    def op(q, f, r, w, sem=None, loose=False, val=16):
+        ops.append({"q": q, "f": f, "r": list(r), "w": list(w), "sem": sem, "loose": loose, "val": val})
+
+    def ts(out, in0, s1, s2, op0, op1, r, w):
+        if op1 is None:
+            op("V", lambda: V.tensor_scalar(out, in0, s1, None, op0), r, w)
+        else:
+            op("V", lambda: V.tensor_scalar(out, in0, s1, s2, op0, op1), r, w)
+
+    def tt(out, in0, in1, o, r, w):
+        op("V", lambda: V.tensor_tensor(out, in0, in1, o), r, w)
+
+    def cp(out, in_, r, w):
+        op("V", lambda: V.tensor_copy(out, in_), r, w)
+
+    def scan(out, d0, d1, init, op0, op1, r, w):
+        op("V", lambda: V.tensor_tensor_scan(out, d0, d1, init, op0, op1), r, w)
+
+    def ms(ap, v, w):
+        op("V", lambda: V.memset(ap, v), [], w)
+
+    def qz(codes, scales, tile, r, w):
+        op("V", lambda: V.quantize_mx(codes, scales, tile), r, w)
+
+    def act(out, in_, func, r, w, bias=0.0, scale=1.0, acc=None):
+        if acc is None:
+            op("S", lambda: S.activation(out, in_, func, bias=bias, scale=scale), r, w)
+        else:
+            op("S", lambda: S.activation(out, in_, func, bias=bias, scale=scale, accum_out=acc), r, w)
+
+    def acp(out, in_, r, w, scale=None):
+        if scale is None:
+            op("S", lambda: S.activation(out, in_, AF.Copy), r, w)
+        else:
+            op("S", lambda: S.activation(out, in_, AF.Copy, scale=scale), r, w)
+
+    def mm(bank, n, lq, lsc, rq, rsc, r):
+        op("P", lambda: g.tensor.matmul_mx(T.ps[:, 512 * bank:512 * bank + n], lq, lsc, rq, rsc, True, True), r, ["ps%d" % bank])
+
+    def iota(out, pattern, base, cm, w, real=False):
+        if real:
+            op("G", lambda: g.iota(out, pattern, base, cm, allow_small_or_imprecise_dtypes=True), [], w)
+        else:
+            op("G", lambda: g.iota(out, pattern, base, cm), [], w)
+
+    sent = [0]
+
+    def send(peer, out, in_, sem, r):
+        rid, pid, _se = topo.addr(peer)
+        sent[0] += len(topo.engines(core, peer))
+        op("G", lambda: g.remote_dma(out, in_, T.sem[sem], T.sem.sent, pid, rid, topo.mask(core, peer)), r, [], loose=True)
+
+    def bank(b, lo=0, hi=C):
+        return T.ps[:, 512 * b + lo:512 * b + hi]
+
+    op("S", lambda: S.dma_start(T.ub[:], T.u[:]), [], ["ub"], sem="lu")
+    op("Y", lambda: g.sync.dma_start(T.win0[:, 0:4 * C], T.x[:]), [], ["T0"], sem="lx")
+    op("Y", lambda: g.sync.dma_start(T.qw[:].bitcast(dt.uint8), T.wc[:]), ["T0"], ["qw"], sem="lwc")
+    op("Y", lambda: g.sync.dma_start(T.sw[:], T.ws[:]), [], ["sw"], sem="lws")
+    op("Y", lambda: g.sync.dma_start(T.vb[:], T.v[:]), [], ["vb"], sem="lv")
+
+    iota(T.i16[:], [[1, 16]], 128, -1, ["i16"])
+    iota(T.ipm[:], [[0, Q]], 0, 1, ["ipm"])
+    iota(T.iou[:], [[1, 2], [16, 8]], 0, 0, ["iou"])
+    iota(T.iid[:], [[1, 128]], 0, -1, ["iid"])
+    iota(T.nb[:], [[16, Q]], 16, 0, ["nb"], real=True)
+    iota(T.one[:], [[1, C]], 1, 0, ["one"], real=True)
+    ms(T.eb[:], 0.0, ["eb0", "eb1", "eb2", "eb3"])
+    ts(T.r16[:], T.i16[:], 15, None, A.bitwise_and, None, ["i16"], ["r16"])
+    ts(T.rpm[:], T.ipm[:], 15, None, A.bitwise_and, None, ["ipm"], ["rpm"])
+    cp(T.ou[:], T.iou[:], ["iou"], ["ou"])
+    ts(T.dm16[:], T.r16[:], 0, None, A.is_equal, None, ["r16"], ["dm16"])
+    cp(T.pm[:], T.rpm[:], ["rpm"], ["pm"])
+    ts(T.kp16[:], T.r16[:], 0, None, A.not_equal, None, ["r16"], ["kp16"])
+    ts(T.t16[:], T.r16[:], 1.0, BIG, A.is_equal, A.mult, ["r16"], ["t16"])
+    ms(T.tab[:, M:C], 0.0, ["tab1"])
+    tt(T.c16[:], T.t16[:], T.kp16[:], A.max, ["t16", "kp16"], ["c16"])
+    for b in range(4):
+        ts(T.eb[:, 512 * b + b:512 * (b + 1):4], T.iid[:], 0, None, A.is_equal, None, ["iid"], ["eb%d" % b])
+    ms(T.tab[:, 0:M], float(C), ["tab0"])
+    ms(T.tab[:, C:C + M], float(C), ["tab2"])
+    acp(T.dm[:], T.dm16[:].indirect(T.pm[:]), ["dm16", "pm"], ["dm"])
+    acp(T.kp[:], T.kp16[:].indirect(T.pm[:]), ["kp16", "pm"], ["kp"])
+    acp(T.cm[:], T.c16[:].indirect(T.pm[:]), ["c16", "pm"], ["cm"])
+    ts(T.inv[:, 0:1], T.dm16[:, 15:16], 1.0 - 1.0 / BIG, 1.0 / BIG, A.mult, A.add, ["dm16"], ["inv0"])
+    ts(T.inv[:, 1:2], T.dm16[:, 15:16], 4.0 - 4.0 / BIG, 4.0 / BIG, A.mult, A.add, ["dm16"], ["inv1"])
+    ts(T.inv[:, 2:3], T.dm16[:, 15:16], 1.0 - BIG, BIG, A.mult, A.add, ["dm16"], ["inv2"])
+    ms(T.b0[:], 1.0, ["b0", "b0b"])
+    ms(T.a0[:, 0:3 * NS:3], 0.0, ["a00"])
+    ms(T.a0[:, 1:3 * NS:3], 1.0, ["a01"])
+    ms(T.a0[:, 2:3 * NS:3], -1.0, ["a02"])
+    ms(T.a1[:], 0.0, ["a1c", "a1h"] + ["a1_%d" % i for i in range(2 * NS)])
+    ms(T.b0[:, 0:4 * Q:4], 0.0, ["b0"])
+    qz(T.qu[:], T.su[:], T.ub[:], ["ub"], ["qu"])
+    cp(T.qp[:].bitcast(dt.uint32), T.qu[:].bitcast(dt.uint32).indirect(T.ou[:]), ["qu", "ou"], ["qp"])
+    acp(T.sp[:], T.su[:].indirect(T.ou[:]), ["qu", "ou"], ["sp"])
+    qz(T.qt0[:], T.sq0[:], T.win0[:, 0:4 * C], ["T0"], ["q0"])
+    qz(T.qe[:], T.se[:], T.eb[:], ["eb0", "eb1", "eb2", "eb3"], ["qe"])
+
+    c0, h = 16 * NV, C // 2
+    for t in range(R):
+        peer = T.cores[rank ^ STEP[t]]
+        ne = len(topo.engines(peer, core))
+        win, nxt = T["win%d" % t], T["win%d" % (t + 1)]
+        qt, sq = T["qt%d" % t], T["sq%d" % t]
+        lq, ls, rk, lr = T["lq%d" % t], T["ls%d" % t], T["rk%d" % t], T["lr%d" % t]
+        kq, kT, kn = "q%d" % t, ["T%d" % t] + ["T%d_%d" % (t, b) for b in range(4)], "T%d" % (t + 1)
+        send(peer, lq[:].bitcast(dt.uint8), qt[:].bitcast(dt.uint8), "ac%d" % t, [kq])
+        send(peer, ls[:], sq[:], "ac%d" % t, [kq])
+        op(None, None, [], ["lq%d" % t], sem="ac%d" % t, val=2 * ne)
+        op(None, None, [], ["lr%d" % t], sem="al%d" % t, val=ne)
+        if t == 0:
+            iota(T.htab[:], [[0, 2], [1, C]], 0, 0, ["htab"], real=True)
+        if t == 1:
+            qz(T.qv[:], T.sv[:], T.vb[:], ["vb"], ["qv"])
+        mm(0, C, T.qp[:, 0:128], T.sp[:, 0:128], qt[:], sq[:], ["qp", "sp", kq])
+        mm(1, C, T.qp[:, 0:128], T.sp[:, 0:128], qt[:], sq[:], ["qp", "sp", kq])
+        mm(2, C, T.qp[:, 128:256], T.sp[:, 128:256], qt[:], sq[:], ["qp", "sp", kq])
+        for b in range(4):
+            mm(4 + b, C, T.qe[:, 128 * b:128 * (b + 1)], T.se[:, 128 * b:128 * (b + 1)], lq[:], ls[:], ["qe", "lq%d" % t])
+        tt(T.mk[:, c0:C], bank(0, c0, C), T.dm[:, c0:C], A.mult, ["ps0", "dm"], ["mk2"])
+        tt(T.mk[:, 0:c0], bank(0, 0, c0), T.dm[:, 0:c0], A.mult, ["ps0", "dm"], ["mk1"])
+        scan(T.hold[:, c0:C], T.kp[:, c0:C], T.mk[:, c0:C], 0.0, A.mult, A.add, ["kp", "mk2"], ["h2"])
+        scan(T.hold[:, 0:c0], T.kp[:, 0:c0], T.mk[:, 0:c0], 0.0, A.mult, A.add, ["kp", "mk1"], ["h1"])
+
+        def sign(i):
+            m = NV + i
+            lo = 16 * (m + 1) if i == 0 else 0
+            act(T.fs[:, i * C + lo:(i + 1) * C], bank(1, lo, C), AF.Sign, ["ps1", "h2"], ["fs%da" % i, "fs%db" % i],
+                bias=T.hold[:, 16 * m + 15:16 * m + 16], scale=-1.0)
+
+        def sums(i):
+            e = 16 * (NV + i + 1)
+            k = PAD + 3 * i
+            if i > 0:
+                a = T.fs[:, i * C:i * C + e]
+                act(a, a, AF.Relu, ["fs%da" % i], ["fs%da" % i, "a1_%d" % (2 * i)], acc=T.a1[:, k + 1:k + 2])
+            if e < C:
+                a = T.fs[:, i * C + e:(i + 1) * C]
+                act(a, a, AF.Relu, ["fs%db" % i], ["fs%db" % i, "a1_%d" % (2 * i + 1)], scale=-1.0, acc=T.a1[:, k + 2:k + 3])
+
+        for i in range(NS):
+            sign(i)
+            if i > 0:
+                sums(i - 1)
+        sums(NS - 1)
+
+        def compare(m):
+            e = 16 * (m + 1)
+            s = T.hold[:, 16 * m + 15:16 * m + 16]
+            ts(T.fv[:, m * C:m * C + e], bank(0, 0, e), s, None, A.is_ge, None, ["ps0", "h1"], ["fv%da" % m])
+            ts(T.fv[:, m * C + e:(m + 1) * C], bank(0, e, C), s, None, A.is_gt, None, ["ps0", "h1"], ["fv%db" % m])
+
+        def total(m):
+            scan(T.zv[:, m * h:(m + 1) * h], T.fv[:, m * C:m * C + h], T.fv[:, m * C + h:(m + 1) * C], T.ci[:, m:m + 1],
+                 A.add, A.add, ["fv%da" % m, "fv%db" % m, "ci"], ["zv%d" % m])
+
+        tt(T.eq[:, c0:C], bank(0, c0, C), T.hold[:, c0:C], A.is_equal, ["ps0", "h2"], ["eq2"])
+        ts(T.fv[:, NV * C:NV * C + 2 * HW], bank(0, 0, 2 * HW), T.hold[:, c0 + 15:c0 + 16], -1.0, A.is_ge, A.mult, ["ps0", "h2"], ["fvh"])
+        tt(T.eq[:, 0:c0], bank(0, 0, c0), T.hold[:, 0:c0], A.is_equal, ["ps0", "h1"], ["eq1"])
+        compare(0)
+        scan(T.cr[:], T.kp[:], T.eq[:], 0.0, A.mult, A.add, ["kp", "eq1", "eq2"], ["cr"])
+        compare(1)
+        ts(T.ci[:, 0:NV], T.cr[:, 15:c0:16], -1.0, -float(h), A.mult, A.add, ["cr"], ["ci"])
+        tt(T.a1[:, PAD + 3:PAD + 3 * NS:3], T.cr[:, c0 + 31:C:16], T.nb[:, NV + 1:Q], A.subtract, ["cr", "nb"], ["a1c"])
+        scan(T.a1[:, PAD - HW + 1:PAD + 1], T.fv[:, NV * C:NV * C + HW], T.fv[:, NV * C + HW:NV * C + 2 * HW],
+             T.cr[:, c0 + 15:c0 + 16], A.add, A.add, ["fvh", "cr"], ["a1h"])
+        total(0)
+        for m in range(2, NV):
+            compare(m)
+            total(m - 1)
+        total(NV - 1)
+        scan(T.ao[:], T.a0[:], T.a1[:, PAD:PAD + 3 * NS], 0.0, A.mult, A.add,
+             ["a00", "a01", "a02", "a1c", "a1h"] + ["a1_%d" % i for i in range(2 * NS)], ["ao"])
+        ts(rk[:, 0:NV], T.zv[:, h - 1:NV * h:h], float(h), None, A.add, None, ["zv%d" % m for m in range(NV)], ["rk%da" % t])
+        cp(rk[:, NV:Q], T.ao[:, 2:3 * NS:3], ["ao"], ["rk%db" % t])
+        kr = ["rk%da" % t, "rk%db" % t]
+        send(peer, lr[:], rk[:], "al%d" % t, kr)
+
+        ts(T.cf[:], bank(2), 0.0, None, A.is_gt, None, ["ps2"], ["cf"])
+        ts(T.b1[:, 2:4 * Q:4], rk[:], -1.0, -1.0, A.mult, A.add, kr, ["b12"])
+        scan(T.cz[:], T.cf[:, 0:h], T.cf[:, h:C], -float(h), A.add, A.add, ["cf"], ["cz"])
+        cp(T.b1[:, 3:4 * Q:4], rk[:], kr, ["b13"])
+        ts(T.st[:, 0:1], T.cz[:, h - 1:h], float(h), float(M), A.add, A.min, ["cz"], ["st0"])
+        ts(T.z16[:], rk[:], T.st[:, 0:1], float(M), A.subtract, A.add, kr + ["st0"], ["z16"])
+        ts(T.lo[:], rk[:], T.st[:, 0:1], None, A.is_lt, None, kr + ["st0"], ["lo"])
+        ts(T.hi[:], rk[:], T.st[:, 0:1], float(L), A.subtract, A.is_ge, kr + ["st0"], ["hi"])
+        ts(T.st[:, 1:2], T.st[:, 0:1], T.inv[:, 2:3], None, A.mult, None, ["st0", "inv2"], ["st1"])
+        tabs = ["tab0", "tab1", "tab2", "z16"]
+        tt(T.val[:], T.tab[:].indirect(T.z16[:]), T.one[:], A.add, tabs + ["one"], ["val"])
+        tt(T.b0[:, 3:4 * Q:4], T.lo[:], T.hi[:], A.add, ["lo", "hi"], ["b0b"])
+        for b in range(4):
+            if b == 2:
+                act(T.nk[:], T.tab[:].indirect(T.z16[:]), AF.Sign, tabs, ["nk"])
+            acp(win[:, 4 * C + b:8 * C:4], bank(4 + b), ["ps%d" % (4 + b)], ["D%d_%d" % (t, b)])
+
+        cp(T.np1[:].indirect(lr[:]), T.nk[:], ["nk", "lr%d" % t], ["np1"])
+        scan(T.tc[:], T.np1[:], T.np1[:], 0.0, A.add, A.max, ["np1"], ["tc"])
+        cp(T.tx[:, 0:h], T.tc[:].indirect(lr[:, 0:Q // 2]), ["tc", "lr%d" % t], ["tx0"])
+        acp(T.tx[:, h:C], T.tc[:].indirect(lr[:, Q // 2:Q]), ["tc", "lr%d" % t], ["tx1"])
+        scan(T.td[:], T.cm[:], T.tx[:], 0.0, A.mult, A.max, ["cm", "tx0", "tx1"], ["td"])
+        ts(T.b1[:, 0:4 * Q:4], T.td[:, 15:C:16], T.inv[:, 0:1], None, A.mult, None, ["td", "inv0"], ["b10"])
+        ts(T.b1[:, 1:4 * Q:4], T.td[:, 15:C:16], T.st[:, 1:2], float(L), A.is_gt, A.mult, ["td", "st1"], ["b11"])
+        scan(T.bo[:], T.b0[:], T.b1[:], 0.0, A.mult, A.add, ["b0", "b0b", "b10", "b11", "b12", "b13"], ["bo"])
+        cp(T.pl[:], T.bo[:, 3:4 * Q:4], ["bo"], ["pl"])
+        cp(T.idx[:].indirect(T.pl[:]), T.val[:], ["val", "pl"], ["idx"])
+        scan(T.idd[:], T.cm[:], T.idx[:], 0.0, A.mult, A.max, ["cm", "idx"], ["idd"])
+        for b in range(4):
+            ts(T.off[:, Q * b:Q * (b + 1)], T.idd[:, 15:C:16], T.inv[:, 1:2], float(b - 4), A.mult, A.add, ["idd", "inv1"], ["off%d" % b])
+        kw = kT + ["D%d_%d" % (t, b) for b in range(4)]
+        for b in range(4):
+            src = win[:].indirect(T.off[:, Q * b:Q * (b + 1)])
+            (acp if b < 2 else cp)(T.ft[:, b:4 * C:4], src, kw + ["off%d" % b], ["ft%d" % b])
+        kf = ["ft%d" % b for b in range(4)]
+        qz(T.qf[:], T.sf[:], T.ft[:], kf, ["qf"])
+        for b in range(4):
+            mm(4 + b, C, T.qw[:, 128 * b:128 * (b + 1)], T.sw[:, 128 * b:128 * (b + 1)], T.qf[:], T.sf[:], ["qw", "sw", "qf"])
+        for b in range(2):
+            acp(T.f64[:, C * b:C * (b + 1)], T.ft[:, b:4 * C:4], ["ft%d" % b], ["f64%d" % b], scale=64.0)
+        for b in range(2, 4):
+            ts(T.f64[:, C * b:C * (b + 1)], T.ft[:, b:4 * C:4], 64.0, None, A.mult, None, ["ft%d" % b], ["f64%d" % b])
+        if t == R - 1:
+            ts(T.off[:, 4 * Q:5 * Q], T.idd[:, 15:C:16], T.inv[:, 0:1], -1.0, A.mult, A.add, ["idd", "inv0"], ["off4"])
+        for b in range(4):
+            tt(T.t64[:, C * b:C * (b + 1)], bank(4 + b), T.f64[:, C * b:C * (b + 1)], A.add, ["ps%d" % (4 + b), "f64%d" % b], ["t64%d" % b])
+        for b in range(3):
+            acp(nxt[:, b:4 * C:4], T.t64[:, C * b:C * (b + 1)], ["t64%d" % b], [kn + "_%d" % b], scale=0.015625)
+        ts(nxt[:, 3:4 * C:4], T.t64[:, 3 * C:4 * C], 0.015625, None, A.mult, None, ["t643"], [kn + "_3"])
+        qz(T["qt%d" % (t + 1)][:], T["sq%d" % (t + 1)][:], nxt[:, 0:4 * C], [kn + "_%d" % b for b in range(4)], ["q%d" % (t + 1)])
+
+    qt, sq, kq = T["qt%d" % R], T["sq%d" % R], "q%d" % R
+    acp(T.hrow[:], T.htab[:].indirect(T.off[:, 4 * Q:5 * Q]), ["htab", "off4"], ["hrow"])
+    mm(0, h, T.qv[:], T.sv[:], qt[:, 0:h], sq[:, 0:h], ["qv", kq])
+    mm(1, h, T.qv[:], T.sv[:], qt[:, h:C], sq[:, h:C], ["qv", kq])
+    cp(T.ys[:, 0:h], bank(0, 0, h), ["ps0"], ["ys0"])
+    acp(T.ys[:, h:C], bank(1, 0, h), ["ps1"], ["ys1"])
+    stores = {"sto": 0, "sty": 0}
+
+    def store(q, sem, out, in_, r):
+        stores[sem] += 16
+        e = g.sync if q == "Y" else S
+        op(q, lambda: e.dma_start(out, in_).then_inc(T.sem[sem], 16), r, [], loose=True)
+
+    store("Y", "sto", T.oc[:], qt[:].bitcast(dt.uint8), [kq])
+    for k in range(4):
+        store("Y", "sto", T.osc[4 * k:4 * k + 4, :], sq[32 * k:32 * k + 4, :], [kq])
+    store("Y", "sto", T.ot[:], T.hrow[0:128:16, :], ["hrow"])
+    store("S", "sty", T.y[:], T.ys[:], ["ys0", "ys1"])
+    schedule(g, T, ops)
+    g.sync.wait_ge(T.sem.sto, stores["sto"])
+    S.wait_ge(T.sem.sty, stores["sty"])
+    g.wait_ge(T.sem.sent, sent[0])

@@ -5,8 +5,8 @@ STEP = [1, 2, 4]
 Q = C // 16
 NV = 14
 NS = Q - NV
-HW = 16 * (NV + 1) // 2
-PAD = HW
+EV, ES = 10, 6
+EQ = EV + ES
 BIG = 1024.0
 X4, BF, F32 = "float8_e4m3fn_x4", "bfloat16", "float32"
 
@@ -16,21 +16,23 @@ for _n, _w, _d in [
         ("qv", 128, X4), ("sv", 128, "uint8"), ("qw", 512, X4), ("sw", 512, "uint8"),
         ("eb", 2048, BF), ("qe", 512, X4), ("se", 512, "uint8"),
         ("i16", 16, "int32"), ("r16", 16, "int32"), ("ipm", Q, "int32"), ("rpm", Q, "int32"), ("pm", Q, "uint16"),
-        ("iou", 16, "int32"), ("ou", 16, "uint16"), ("iid", 128, "int32"),
+        ("iou", 16, "int32"), ("ou", 16, "uint16"), ("iid", 128, "int32"), ("i24", Q, "int32"), ("x24", Q, F32),
         ("dm16", 16, F32), ("kp16", 16, F32), ("t16", 16, F32), ("c16", 16, F32),
-        ("dm", C, F32), ("kp", C, BF), ("cm", C, BF), ("inv", 4, F32), ("one", C, F32), ("nb", Q, F32),
+        ("dm", C, F32), ("kp", C, BF), ("cm", C, BF), ("inv", 4, F32), ("vtab", 2 * C, F32), ("nb", Q, F32),
         ("tab", C + M, BF), ("htab", 2 * C, F32),
         ("mk", C, F32), ("hold", C, F32), ("eq", C, BF), ("cr", C, BF), ("ci", Q, F32),
-        ("fv", (NV + 1) * C, BF), ("zv", NV * C // 2, BF), ("fs", NS * C, BF),
-        ("a0", 3 * NS, F32), ("a1", PAD + 3 * NS, F32), ("ao", 3 * NS, F32),
-        ("cf", C, BF), ("cz", C // 2, BF), ("st", 4, F32), ("z16", Q, "uint16"), ("lo", Q, F32), ("hi", Q, F32),
+        ("fv", NV * C, BF), ("zv", NV * C // 2, BF), ("fs", NS * C, BF),
+        ("a0", 3 * NS, F32), ("a1", 3 * NS, F32), ("ao", 3 * NS, F32),
+        ("cf", C, BF), ("st", 4, F32), ("z16", Q, "uint16"), ("lo", Q, F32), ("hi", Q, F32),
+        ("v1", Q, F32), ("v2", Q, F32), ("v16", Q, "uint16"),
         ("b0", 4 * Q, F32), ("b1", 4 * Q, F32), ("bo", 4 * Q, F32),
         ("nk", C, BF), ("val", C, F32), ("np1", C, BF), ("tc", C, BF), ("tx", C, BF), ("td", C, BF),
-        ("pl", Q, "uint16"), ("idx", C, F32), ("idd", C, F32), ("off", 5 * Q, "uint16"), ("hrow", C, F32),
-        ("ft", 4 * C, BF), ("f64", 4 * C, BF), ("t64", 4 * C, BF), ("qf", C, X4), ("sf", C, "uint8"), ("ys", C, F32)]:
+        ("pl", Q, "uint16"), ("idx", C, F32), ("idd", C, F32), ("off", Q, "uint16"), ("hrow", C, F32),
+        ("ft", 4 * C, BF), ("f64", 4 * C, BF), ("qf", C, X4), ("sf", C, "uint8"), ("ys", C, F32)]:
     SCRATCH[_n] = ("sbuf", [128, _w], _d)
 for _t in range(R + 1):
-    SCRATCH["win%d" % _t] = ("sbuf", [128, (8 if _t < R else 4) * C], BF)
+    SCRATCH["win%d" % _t] = ("sbuf", [128, 8 * C], BF)
+    SCRATCH["tt%d" % _t] = ("sbuf", [128, 4 * C], BF)
     SCRATCH["qt%d" % _t] = ("sbuf", [128, C], X4)
     SCRATCH["sq%d" % _t] = ("sbuf", [128, C], "uint8")
 for _t in range(R):
@@ -40,7 +42,7 @@ for _t in range(R):
     SCRATCH["lr%d" % _t] = ("sbuf", [128, Q], "uint16")
 
 SEMAPHORES = ["V", "S", "P", "G", "lx", "lu", "lv", "lwc", "lws", "sent", "sty", "sto",
-              "ac0", "ac1", "ac2", "al0", "al1", "al2"]
+              "ac0", "ac1", "ac2", "ae0", "ae1", "ae2", "al0", "al1", "al2"]
 
 
 def schedule(g, T, ops):
@@ -162,7 +164,7 @@ def rank_program(g, core, T, topo):
         return T.ps[:, 512 * b + lo:512 * b + hi]
 
     op("S", lambda: S.dma_start(T.ub[:], T.u[:]), [], ["ub"], sem="lu")
-    op("Y", lambda: g.sync.dma_start(T.win0[:, 0:4 * C], T.x[:]), [], ["T0"], sem="lx")
+    op("Y", lambda: g.sync.dma_start(T.tt0[:], T.x[:]), [], ["T0"], sem="lx")
     op("Y", lambda: g.sync.dma_start(T.qw[:].bitcast(dt.uint8), T.wc[:]), ["T0"], ["qw"], sem="lwc")
     op("Y", lambda: g.sync.dma_start(T.sw[:], T.ws[:]), [], ["sw"], sem="lws")
     op("Y", lambda: g.sync.dma_start(T.vb[:], T.v[:]), [], ["vb"], sem="lv")
@@ -172,7 +174,9 @@ def rank_program(g, core, T, topo):
     iota(T.iou[:], [[1, 2], [16, 8]], 0, 0, ["iou"])
     iota(T.iid[:], [[1, 128]], 0, -1, ["iid"])
     iota(T.nb[:], [[16, Q]], 16, 0, ["nb"], real=True)
-    iota(T.one[:], [[1, C]], 1, 0, ["one"], real=True)
+    iota(T.i24[:, 0:EV], [[16, EV]], 0, 0, ["i24a"])
+    iota(T.i24[:, EV:EQ], [[16, ES]], 16 * (Q - ES), 0, ["i24b"])
+    iota(T.i24[:, EQ:Q], [[16, Q - EQ]], 16 * EV, 0, ["i24c"])
     ms(T.eb[:], 0.0, ["eb0", "eb1", "eb2", "eb3"])
     ts(T.r16[:], T.i16[:], 15, None, A.bitwise_and, None, ["i16"], ["r16"])
     ts(T.rpm[:], T.ipm[:], 15, None, A.bitwise_and, None, ["ipm"], ["rpm"])
@@ -185,73 +189,82 @@ def rank_program(g, core, T, topo):
     tt(T.c16[:], T.t16[:], T.kp16[:], A.max, ["t16", "kp16"], ["c16"])
     for b in range(4):
         ts(T.eb[:, 512 * b + b:512 * (b + 1):4], T.iid[:], 0, None, A.is_equal, None, ["iid"], ["eb%d" % b])
-    ms(T.tab[:, 0:M], float(C), ["tab0"])
-    ms(T.tab[:, C:C + M], float(C), ["tab2"])
+    ms(T.tab[:, 0:M], 1.0, ["tab0"])
+    ms(T.tab[:, C:C + M], 1.0, ["tab2"])
     acp(T.dm[:], T.dm16[:].indirect(T.pm[:]), ["dm16", "pm"], ["dm"])
     acp(T.kp[:], T.kp16[:].indirect(T.pm[:]), ["kp16", "pm"], ["kp"])
     acp(T.cm[:], T.c16[:].indirect(T.pm[:]), ["c16", "pm"], ["cm"])
     ts(T.inv[:, 0:1], T.dm16[:, 15:16], 1.0 - 1.0 / BIG, 1.0 / BIG, A.mult, A.add, ["dm16"], ["inv0"])
-    ts(T.inv[:, 1:2], T.dm16[:, 15:16], 4.0 - 4.0 / BIG, 4.0 / BIG, A.mult, A.add, ["dm16"], ["inv1"])
-    ts(T.inv[:, 2:3], T.dm16[:, 15:16], 1.0 - BIG, BIG, A.mult, A.add, ["dm16"], ["inv2"])
+    ts(T.inv[:, 2:3], T.dm16[:, 15:16], BIG - 1.0, -BIG, A.mult, A.add, ["dm16"], ["inv2"])
     ms(T.b0[:], 1.0, ["b0", "b0b"])
     ms(T.a0[:, 0:3 * NS:3], 0.0, ["a00"])
     ms(T.a0[:, 1:3 * NS:3], 1.0, ["a01"])
     ms(T.a0[:, 2:3 * NS:3], -1.0, ["a02"])
-    ms(T.a1[:], 0.0, ["a1c", "a1h"] + ["a1_%d" % i for i in range(2 * NS)])
+    ms(T.a1[:], 0.0, ["a1c"] + ["a1_%d" % i for i in range(2 * NS)])
     ms(T.b0[:, 0:4 * Q:4], 0.0, ["b0"])
+    tt(T.x24[:], T.i24[:], T.rpm[:], A.add, ["i24a", "i24b", "i24c", "rpm"], ["x24"])
     qz(T.qu[:], T.su[:], T.ub[:], ["ub"], ["qu"])
     cp(T.qp[:].bitcast(dt.uint32), T.qu[:].bitcast(dt.uint32).indirect(T.ou[:]), ["qu", "ou"], ["qp"])
     acp(T.sp[:], T.su[:].indirect(T.ou[:]), ["qu", "ou"], ["sp"])
-    qz(T.qt0[:], T.sq0[:], T.win0[:, 0:4 * C], ["T0"], ["q0"])
+    qz(T.qt0[:], T.sq0[:], T.tt0[:], ["T0"], ["q0"])
     qz(T.qe[:], T.se[:], T.eb[:], ["eb0", "eb1", "eb2", "eb3"], ["qe"])
 
-    c0, h = 16 * NV, C // 2
+    def plane0(b):
+        acp(T.win0[:, 2 * C * b:2 * C * b + C], T.tt0[:, b:4 * C:4], ["T0"], ["W0_%d" % b], scale=64.0)
+
+    plane0(0)
+    plane0(1)
+
+    c0, h, e0 = 16 * NV, C // 2, 16 * EQ
     for t in range(R):
         peer = T.cores[rank ^ STEP[t]]
         ne = len(topo.engines(peer, core))
-        win, nxt = T["win%d" % t], T["win%d" % (t + 1)]
+        win, nxt, tile = T["win%d" % t], T["win%d" % (t + 1)], T["tt%d" % (t + 1)]
         qt, sq = T["qt%d" % t], T["sq%d" % t]
         lq, ls, rk, lr = T["lq%d" % t], T["ls%d" % t], T["rk%d" % t], T["lr%d" % t]
-        kq, kT, kn = "q%d" % t, ["T%d" % t] + ["T%d_%d" % (t, b) for b in range(4)], "T%d" % (t + 1)
+        kq, kn = "q%d" % t, "T%d" % (t + 1)
+        le, ll = "le%d" % t, "ll%d" % t
         send(peer, lq[:].bitcast(dt.uint8), qt[:].bitcast(dt.uint8), "ac%d" % t, [kq])
         send(peer, ls[:], sq[:], "ac%d" % t, [kq])
         op(None, None, [], ["lq%d" % t], sem="ac%d" % t, val=2 * ne)
-        op(None, None, [], ["lr%d" % t], sem="al%d" % t, val=ne)
+        op(None, None, [], [le], sem="ae%d" % t, val=ne)
+        op(None, None, [], [ll], sem="al%d" % t, val=ne)
         if t == 0:
+            iota(T.vtab[:], [[1, 2 * C]], 1, 0, ["vtab"], real=True)
             iota(T.htab[:], [[0, 2], [1, C]], 0, 0, ["htab"], real=True)
         if t == 1:
             qz(T.qv[:], T.sv[:], T.vb[:], ["vb"], ["qv"])
         mm(0, C, T.qp[:, 0:128], T.sp[:, 0:128], qt[:], sq[:], ["qp", "sp", kq])
-        mm(1, C, T.qp[:, 0:128], T.sp[:, 0:128], qt[:], sq[:], ["qp", "sp", kq])
         mm(2, C, T.qp[:, 128:256], T.sp[:, 128:256], qt[:], sq[:], ["qp", "sp", kq])
+        mm(1, C, T.qp[:, 0:128], T.sp[:, 0:128], qt[:], sq[:], ["qp", "sp", kq])
         for b in range(4):
             mm(4 + b, C, T.qe[:, 128 * b:128 * (b + 1)], T.se[:, 128 * b:128 * (b + 1)], lq[:], ls[:], ["qe", "lq%d" % t])
         tt(T.mk[:, c0:C], bank(0, c0, C), T.dm[:, c0:C], A.mult, ["ps0", "dm"], ["mk2"])
         tt(T.mk[:, 0:c0], bank(0, 0, c0), T.dm[:, 0:c0], A.mult, ["ps0", "dm"], ["mk1"])
         scan(T.hold[:, c0:C], T.kp[:, c0:C], T.mk[:, c0:C], 0.0, A.mult, A.add, ["kp", "mk2"], ["h2"])
         scan(T.hold[:, 0:c0], T.kp[:, 0:c0], T.mk[:, 0:c0], 0.0, A.mult, A.add, ["kp", "mk1"], ["h1"])
+        act(T.cf[:], bank(2), AF.Sign, ["ps2"], ["cf"])
 
         def sign(i):
             m = NV + i
-            lo = 16 * (m + 1) if i == 0 else 0
-            act(T.fs[:, i * C + lo:(i + 1) * C], bank(1, lo, C), AF.Sign, ["ps1", "h2"], ["fs%da" % i, "fs%db" % i],
+            act(T.fs[:, i * C:(i + 1) * C], bank(1), AF.Sign, ["ps1", "h2"], ["fs%da" % i, "fs%db" % i],
                 bias=T.hold[:, 16 * m + 15:16 * m + 16], scale=-1.0)
 
         def sums(i):
             e = 16 * (NV + i + 1)
-            k = PAD + 3 * i
-            if i > 0:
-                a = T.fs[:, i * C:i * C + e]
-                act(a, a, AF.Relu, ["fs%da" % i], ["fs%da" % i, "a1_%d" % (2 * i)], acc=T.a1[:, k + 1:k + 2])
+            a = T.fs[:, i * C:i * C + e]
+            act(a, a, AF.Relu, ["fs%da" % i], ["fs%da" % i, "a1_%d" % (2 * i)], acc=T.a1[:, 3 * i + 1:3 * i + 2])
             if e < C:
                 a = T.fs[:, i * C + e:(i + 1) * C]
-                act(a, a, AF.Relu, ["fs%db" % i], ["fs%db" % i, "a1_%d" % (2 * i + 1)], scale=-1.0, acc=T.a1[:, k + 2:k + 3])
+                act(a, a, AF.Relu, ["fs%db" % i], ["fs%db" % i, "a1_%d" % (2 * i + 1)], scale=-1.0, acc=T.a1[:, 3 * i + 2:3 * i + 3])
 
-        for i in range(NS):
+        for i in range(NS - 1, -1, -1):
             sign(i)
-            if i > 0:
-                sums(i - 1)
-        sums(NS - 1)
+            if i < NS - 1:
+                sums(i + 1)
+        sums(0)
+        act(T.cf[:], T.cf[:], AF.Relu, ["cf"], ["cf", "st0"], acc=T.st[:, 0:1])
+        act(T.st[:, 1:2], T.st[:, 0:1], AF.Relu, ["st0"], ["st1"], bias=float(M), scale=-1.0)
 
         def compare(m):
             e = 16 * (m + 1)
@@ -263,62 +276,88 @@ def rank_program(g, core, T, topo):
             scan(T.zv[:, m * h:(m + 1) * h], T.fv[:, m * C:m * C + h], T.fv[:, m * C + h:(m + 1) * C], T.ci[:, m:m + 1],
                  A.add, A.add, ["fv%da" % m, "fv%db" % m, "ci"], ["zv%d" % m])
 
+        def fold(i0, i1, key):
+            scan(T.ao[:, 3 * i0:3 * i1], T.a0[:, 3 * i0:3 * i1], T.a1[:, 3 * i0:3 * i1], 0.0, A.mult, A.add,
+                 ["a00", "a01", "a02", "a1c"] + ["a1_%d" % i for i in range(2 * i0, 2 * i1)], [key])
+
+        def places(at, m0, m1, key):
+            ts(rk[:, at:at + m1 - m0], T.zv[:, (m0 + 1) * h - 1:m1 * h:h], float(h), None, A.add, None,
+               ["zv%d" % m for m in range(m0, m1)], [key])
+
         tt(T.eq[:, c0:C], bank(0, c0, C), T.hold[:, c0:C], A.is_equal, ["ps0", "h2"], ["eq2"])
-        ts(T.fv[:, NV * C:NV * C + 2 * HW], bank(0, 0, 2 * HW), T.hold[:, c0 + 15:c0 + 16], -1.0, A.is_ge, A.mult, ["ps0", "h2"], ["fvh"])
         tt(T.eq[:, 0:c0], bank(0, 0, c0), T.hold[:, 0:c0], A.is_equal, ["ps0", "h1"], ["eq1"])
         compare(0)
         scan(T.cr[:], T.kp[:], T.eq[:], 0.0, A.mult, A.add, ["kp", "eq1", "eq2"], ["cr"])
         compare(1)
         ts(T.ci[:, 0:NV], T.cr[:, 15:c0:16], -1.0, -float(h), A.mult, A.add, ["cr"], ["ci"])
-        tt(T.a1[:, PAD + 3:PAD + 3 * NS:3], T.cr[:, c0 + 31:C:16], T.nb[:, NV + 1:Q], A.subtract, ["cr", "nb"], ["a1c"])
-        scan(T.a1[:, PAD - HW + 1:PAD + 1], T.fv[:, NV * C:NV * C + HW], T.fv[:, NV * C + HW:NV * C + 2 * HW],
-             T.cr[:, c0 + 15:c0 + 16], A.add, A.add, ["fvh", "cr"], ["a1h"])
+        tt(T.a1[:, 0:3 * NS:3], T.cr[:, c0 + 15:C:16], T.nb[:, NV:Q], A.subtract, ["cr", "nb"], ["a1c"])
+        compare(2)
         total(0)
-        for m in range(2, NV):
+        total(1)
+        kr = ["rk%d%s" % (t, n) for n in "abcd"]
+        for m in range(3, NV):
             compare(m)
+            if m == EV + 1:
+                places(0, 0, EV, kr[0])
+                cp(rk[:, EV:EQ], T.ao[:, 3 * (NS - ES) + 2:3 * NS:3], ["aoe"], [kr[1]])
+                send(peer, lr[:, 0:EQ], rk[:, 0:EQ], "ae%d" % t, kr[0:2])
             total(m - 1)
+            if m == EV:
+                fold(NS - ES, NS, "aoe")
         total(NV - 1)
-        scan(T.ao[:], T.a0[:], T.a1[:, PAD:PAD + 3 * NS], 0.0, A.mult, A.add,
-             ["a00", "a01", "a02", "a1c", "a1h"] + ["a1_%d" % i for i in range(2 * NS)], ["ao"])
-        ts(rk[:, 0:NV], T.zv[:, h - 1:NV * h:h], float(h), None, A.add, None, ["zv%d" % m for m in range(NV)], ["rk%da" % t])
-        cp(rk[:, NV:Q], T.ao[:, 2:3 * NS:3], ["ao"], ["rk%db" % t])
-        kr = ["rk%da" % t, "rk%db" % t]
-        send(peer, lr[:], rk[:], "al%d" % t, kr)
+        fold(0, NS - ES, "aol")
+        places(EQ, EV, NV, kr[2])
+        cp(rk[:, EQ + NV - EV:Q], T.ao[:, 2:3 * (NS - ES):3], ["aol"], [kr[3]])
+        send(peer, lr[:, EQ:Q], rk[:, EQ:Q], "al%d" % t, kr[2:4])
 
-        ts(T.cf[:], bank(2), 0.0, None, A.is_gt, None, ["ps2"], ["cf"])
+        r = T.st[:, 1:2]
+        ts(T.z16[:, 0:EQ], rk[:, 0:EQ], r, None, A.add, None, kr[0:2] + ["st1"], ["ze"])
+        ts(T.z16[:, EQ:Q], rk[:, EQ:Q], r, None, A.add, None, kr[2:4] + ["st1"], ["zl"])
+        ts(T.lo[:], rk[:], r, float(M), A.add, A.is_lt, kr + ["st1"], ["lo"])
+        ts(T.hi[:], rk[:], r, float(C), A.add, A.is_ge, kr + ["st1"], ["hi"])
         ts(T.b1[:, 2:4 * Q:4], rk[:], -1.0, -1.0, A.mult, A.add, kr, ["b12"])
-        scan(T.cz[:], T.cf[:, 0:h], T.cf[:, h:C], -float(h), A.add, A.add, ["cf"], ["cz"])
-        cp(T.b1[:, 3:4 * Q:4], rk[:], kr, ["b13"])
-        ts(T.st[:, 0:1], T.cz[:, h - 1:h], float(h), float(M), A.add, A.min, ["cz"], ["st0"])
-        ts(T.z16[:], rk[:], T.st[:, 0:1], float(M), A.subtract, A.add, kr + ["st0"], ["z16"])
-        ts(T.lo[:], rk[:], T.st[:, 0:1], None, A.is_lt, None, kr + ["st0"], ["lo"])
-        ts(T.hi[:], rk[:], T.st[:, 0:1], float(L), A.subtract, A.is_ge, kr + ["st0"], ["hi"])
-        ts(T.st[:, 1:2], T.st[:, 0:1], T.inv[:, 2:3], None, A.mult, None, ["st0", "inv2"], ["st1"])
-        tabs = ["tab0", "tab1", "tab2", "z16"]
-        tt(T.val[:], T.tab[:].indirect(T.z16[:]), T.one[:], A.add, tabs + ["one"], ["val"])
         tt(T.b0[:, 3:4 * Q:4], T.lo[:], T.hi[:], A.add, ["lo", "hi"], ["b0b"])
-        for b in range(4):
-            if b == 2:
-                act(T.nk[:], T.tab[:].indirect(T.z16[:]), AF.Sign, tabs, ["nk"])
-            acp(win[:, 4 * C + b:8 * C:4], bank(4 + b), ["ps%d" % (4 + b)], ["D%d_%d" % (t, b)])
+        cp(T.b1[:, 3:4 * Q:4], rk[:], kr, ["b13"])
+        ts(T.v1[:], T.b0[:, 3:4 * Q:4], float(C), None, A.mult, None, ["b0b"], ["v1"])
+        tabs = ["tab0", "tab1", "tab2"]
 
-        cp(T.np1[:].indirect(lr[:]), T.nk[:], ["nk", "lr%d" % t], ["np1"])
+        def unpack(b):
+            acp(win[:, 2 * C * b + C:2 * C * (b + 1)], bank(4 + b), ["ps%d" % (4 + b)], ["D%d_%d" % (t, b)], scale=64.0)
+
+        acp(T.nk[:, 0:e0], T.tab[:].indirect(T.z16[:, 0:EQ]), tabs + ["ze"], ["nke"])
+        acp(T.nk[:, e0:C], T.tab[:].indirect(T.z16[:, EQ:Q]), tabs + ["zl"], ["nkl"])
+        unpack(0)
+        unpack(1)
+
+        cp(T.np1[:].indirect(lr[:, 0:EQ]), T.nk[:, 0:e0], ["nke", le], ["np1"])
+        tt(T.v2[:], T.v1[:], T.x24[:], A.add, ["v1", "x24"], ["v2"])
+        ts(T.st[:, 2:3], r, -float(M), T.inv[:, 2:3], A.add, A.mult, ["st1", "inv2"], ["st2"])
+        cp(T.v16[:], T.v2[:], ["v2"], ["v16"])
+        cp(T.np1[:].indirect(lr[:, EQ:Q]), T.nk[:, e0:C], ["nkl", ll], ["np1"])
         scan(T.tc[:], T.np1[:], T.np1[:], 0.0, A.add, A.max, ["np1"], ["tc"])
-        cp(T.tx[:, 0:h], T.tc[:].indirect(lr[:, 0:Q // 2]), ["tc", "lr%d" % t], ["tx0"])
-        acp(T.tx[:, h:C], T.tc[:].indirect(lr[:, Q // 2:Q]), ["tc", "lr%d" % t], ["tx1"])
+        cp(T.tx[:, 0:h], T.tc[:].indirect(lr[:, 0:Q // 2]), ["tc", le, ll], ["tx0"])
+        acp(T.tx[:, h:C], T.tc[:].indirect(lr[:, Q // 2:Q]), ["tc", le, ll], ["tx1"])
+        acp(T.val[:], T.vtab[:].indirect(T.v16[:]), ["vtab", "v16"], ["val"])
+        unpack(2)
+        unpack(3)
+        if t == 0:
+            plane0(2)
+            plane0(3)
         scan(T.td[:], T.cm[:], T.tx[:], 0.0, A.mult, A.max, ["cm", "tx0", "tx1"], ["td"])
         ts(T.b1[:, 0:4 * Q:4], T.td[:, 15:C:16], T.inv[:, 0:1], None, A.mult, None, ["td", "inv0"], ["b10"])
-        ts(T.b1[:, 1:4 * Q:4], T.td[:, 15:C:16], T.st[:, 1:2], float(L), A.is_gt, A.mult, ["td", "st1"], ["b11"])
+        ts(T.b1[:, 1:4 * Q:4], T.td[:, 15:C:16], T.st[:, 2:3], float(L), A.is_gt, A.mult, ["td", "st2"], ["b11"])
         scan(T.bo[:], T.b0[:], T.b1[:], 0.0, A.mult, A.add, ["b0", "b0b", "b10", "b11", "b12", "b13"], ["bo"])
         cp(T.pl[:], T.bo[:, 3:4 * Q:4], ["bo"], ["pl"])
         cp(T.idx[:].indirect(T.pl[:]), T.val[:], ["val", "pl"], ["idx"])
         scan(T.idd[:], T.cm[:], T.idx[:], 0.0, A.mult, A.max, ["cm", "idx"], ["idd"])
+        ts(T.off[:], T.idd[:, 15:C:16], T.inv[:, 0:1], -1.0, A.mult, A.add, ["idd", "inv0"], ["off"])
         for b in range(4):
-            ts(T.off[:, Q * b:Q * (b + 1)], T.idd[:, 15:C:16], T.inv[:, 1:2], float(b - 4), A.mult, A.add, ["idd", "inv1"], ["off%d" % b])
-        kw = kT + ["D%d_%d" % (t, b) for b in range(4)]
-        for b in range(4):
-            src = win[:].indirect(T.off[:, Q * b:Q * (b + 1)])
-            (acp if b < 2 else cp)(T.ft[:, b:4 * C:4], src, kw + ["off%d" % b], ["ft%d" % b])
+            src = win[:, 2 * C * b:2 * C * (b + 1)].indirect(T.off[:])
+            kw = ["W%d_%d" % (t, b), "D%d_%d" % (t, b), "off"]
+            if b < 2:
+                acp(T.ft[:, b:4 * C:4], src, kw, ["ft%d" % b], scale=0.015625)
+            else:
+                ts(T.ft[:, b:4 * C:4], src, 0.015625, None, A.mult, None, kw, ["ft%d" % b])
         kf = ["ft%d" % b for b in range(4)]
         qz(T.qf[:], T.sf[:], T.ft[:], kf, ["qf"])
         for b in range(4):
@@ -327,17 +366,16 @@ def rank_program(g, core, T, topo):
             acp(T.f64[:, C * b:C * (b + 1)], T.ft[:, b:4 * C:4], ["ft%d" % b], ["f64%d" % b], scale=64.0)
         for b in range(2, 4):
             ts(T.f64[:, C * b:C * (b + 1)], T.ft[:, b:4 * C:4], 64.0, None, A.mult, None, ["ft%d" % b], ["f64%d" % b])
-        if t == R - 1:
-            ts(T.off[:, 4 * Q:5 * Q], T.idd[:, 15:C:16], T.inv[:, 0:1], -1.0, A.mult, A.add, ["idd", "inv0"], ["off4"])
         for b in range(4):
-            tt(T.t64[:, C * b:C * (b + 1)], bank(4 + b), T.f64[:, C * b:C * (b + 1)], A.add, ["ps%d" % (4 + b), "f64%d" % b], ["t64%d" % b])
+            tt(nxt[:, 2 * C * b:2 * C * b + C], bank(4 + b), T.f64[:, C * b:C * (b + 1)], A.add,
+               ["ps%d" % (4 + b), "f64%d" % b], ["W%d_%d" % (t + 1, b)])
         for b in range(3):
-            acp(nxt[:, b:4 * C:4], T.t64[:, C * b:C * (b + 1)], ["t64%d" % b], [kn + "_%d" % b], scale=0.015625)
-        ts(nxt[:, 3:4 * C:4], T.t64[:, 3 * C:4 * C], 0.015625, None, A.mult, None, ["t643"], [kn + "_3"])
-        qz(T["qt%d" % (t + 1)][:], T["sq%d" % (t + 1)][:], nxt[:, 0:4 * C], [kn + "_%d" % b for b in range(4)], ["q%d" % (t + 1)])
+            acp(tile[:, b:4 * C:4], nxt[:, 2 * C * b:2 * C * b + C], ["W%d_%d" % (t + 1, b)], [kn + "_%d" % b], scale=0.015625)
+        ts(tile[:, 3:4 * C:4], nxt[:, 6 * C:7 * C], 0.015625, None, A.mult, None, ["W%d_3" % (t + 1)], [kn + "_3"])
+        qz(T["qt%d" % (t + 1)][:], T["sq%d" % (t + 1)][:], tile[:], [kn + "_%d" % b for b in range(4)], ["q%d" % (t + 1)])
 
     qt, sq, kq = T["qt%d" % R], T["sq%d" % R], "q%d" % R
-    acp(T.hrow[:], T.htab[:].indirect(T.off[:, 4 * Q:5 * Q]), ["htab", "off4"], ["hrow"])
+    acp(T.hrow[:], T.htab[:].indirect(T.off[:]), ["htab", "off"], ["hrow"])
     mm(0, h, T.qv[:], T.sv[:], qt[:, 0:h], sq[:, 0:h], ["qv", kq])
     mm(1, h, T.qv[:], T.sv[:], qt[:, h:C], sq[:, h:C], ["qv", kq])
     cp(T.ys[:, 0:h], bank(0, 0, h), ["ps0"], ["ys0"])

@@ -3,26 +3,37 @@ from concourse.mybir import dt, AluOpType as A, ActivationFunctionType as AF
 C, L, M, R = 384, 160, 224, 3
 STEP = [1, 2, 4]
 Q = C // 16
-NV = 14
-NS = Q - NV
-EV, ES = 10, 6
-EQ = EV + ES
-BIG = 1024.0
+H = C // 2
+K = Q // 2
+W = 8 * (Q - 1)
+BIG, LOCK, FAR = 1024.0, 4096.0, 1e29
 X4, BF, F32 = "float8_e4m3fn_x4", "bfloat16", "float32"
+QUADS = [[12, 23, 22, 21], [20, 19, 18, 17], [16, 15, 14, 13], [0, 11, 10, 9], [8, 7, 6, 5], [4, 3, 2, 1]]
+WIDE = [C, 320, 256, 192, 128, 64]
+AT = [sum(WIDE[:a]) for a in range(len(WIDE) + 1)]
+NF = AT[-1] + 64
+RUNS = {"A": [[8, 9, 10, 11]], "B": [[13, 15, 17, 19, 21, 23]]}
+LAYER = ("gA2V gA0S gA3V gA1S gB2V gB0S qfA wA gB3V gB1S qfB wB fA0S fA1S fA2S fA3S fB0S fB1S fB2V fB3V tA0 tA1 tA2 tA3 lA0S lA1S lA2S "
+         "tB0 lA3V tB1 lB0S lB1S qA pA yA tB2 tB3 lB2S lB3S mkA ya hrow qB send pF yB yb hdA").split()
+COUNT = ("a11 a10 b11 b10 a9 a8 b9 b8 ownA c7 c6 c5 mkB crA c4 c3 hdB ciA c2 c1 "
+         "a23 a21 b23 b21 a19 a17 b19 b17 a15 a13 b15 b13 n1 n2 n3 "
+         "c22 ownB c12 c20 crB c18 ciB q01 c16 c14 q36 s22 q12 s20 s18 s16 q23 s14 s12 fB s7 s6 xB s5 s4 s3 dB s2 s1 f0 fA rB xA "
+         "zB dA rA").split()
 
 SCRATCH = {"ps": ("psum", [128, 4096], F32)}
 for _n, _w, _d in [
         ("ub", 512, BF), ("vb", 512, BF), ("qu", 128, X4), ("su", 128, "uint8"), ("qp", 256, X4), ("sp", 256, "uint8"),
         ("qv", 128, X4), ("sv", 128, "uint8"), ("qw", 512, X4), ("sw", 512, "uint8"),
-        ("eb", 2048, BF), ("qe", 512, X4), ("se", 512, "uint8"),
+        ("eb", 1056, BF), ("qe", 512, X4), ("se", 512, "uint8"), ("one", 514, BF), ("gb", 512, BF), ("gs", 512, BF),
+        ("qg", 128, X4), ("sg", 128, "uint8"),
         ("i16", 16, "int32"), ("r16", 16, "int32"), ("ipm", Q, "int32"), ("rpm", Q, "int32"), ("pm", Q, "uint16"),
-        ("iou", 16, "int32"), ("ou", 16, "uint16"), ("iid", 128, "int32"), ("i24", Q, "int32"), ("x24", Q, F32),
-        ("dm16", 16, F32), ("kp16", 16, F32), ("t16", 16, F32), ("c16", 16, F32),
-        ("dm", C, F32), ("kp", C, BF), ("cm", C, BF), ("inv", 4, F32), ("vtab", 2 * C, F32), ("nb", Q, F32),
+        ("iou", 16, "int32"), ("ou", 16, "uint16"), ("i24", Q, "int32"), ("x24", Q, F32), ("ca", Q, F32),
+        ("dm16", 16, F32), ("kp16", 16, F32), ("t16", 16, F32), ("c16", 16, F32), ("m16", 16, F32), ("n16", 16, F32),
+        ("l16", 16, F32), ("e16", 16, F32), ("a16", 16, F32),
+        ("am", C, F32), ("km", C, F32), ("ad", C, F32), ("kp", C, BF), ("cm", C, BF), ("inv", 4, F32), ("vtab", 2 * C, F32),
         ("tab", C + M, BF), ("htab", 2 * C, F32),
-        ("mk", C, F32), ("hold", C, F32), ("eq", C, BF), ("cr", C, BF), ("ci", Q, F32),
-        ("fv", NV * C, BF), ("zv", NV * C // 2, BF), ("fs", NS * C, BF),
-        ("a0", 3 * NS, F32), ("a1", 3 * NS, F32), ("ao", 3 * NS, F32),
+        ("mk", C, F32), ("hold", C, F32), ("cr", C, BF), ("ci", Q, F32), ("acc", Q, F32),
+        ("fl", 4 * NF, BF), ("qc", NF, X4), ("sc", NF, "uint8"), ("zv", Q * W, BF), ("fs", Q * C, BF), ("cd", C, F32),
         ("cf", C, BF), ("st", 4, F32), ("z16", Q, "uint16"), ("lo", Q, F32), ("hi", Q, F32),
         ("v1", Q, F32), ("v2", Q, F32), ("v16", Q, "uint16"),
         ("b0", 4 * Q, F32), ("b1", 4 * Q, F32), ("bo", 4 * Q, F32),
@@ -39,31 +50,35 @@ for _t in range(R):
     SCRATCH["lq%d" % _t] = ("sbuf", [128, C], X4)
     SCRATCH["ls%d" % _t] = ("sbuf", [128, C], "uint8")
     SCRATCH["rk%d" % _t] = ("sbuf", [128, Q], "uint16")
-    SCRATCH["lr%d" % _t] = ("sbuf", [128, Q], "uint16")
+    SCRATCH["lA%d" % _t] = ("sbuf", [128, K], "uint16")
+    SCRATCH["lB%d" % _t] = ("sbuf", [128, K], "uint16")
 
-SEMAPHORES = ["V", "S", "P", "G", "lx", "lu", "lv", "lwc", "lws", "sent", "sty", "sto",
-              "ac0", "ac1", "ac2", "ae0", "ae1", "ae2", "al0", "al1", "al2"]
+SEMAPHORES = ["V", "S", "P", "G", "lxA", "lxB", "lu", "lv", "lwc", "lws", "sent", "sty", "sto",
+              "ac0", "ac1", "ac2", "aA0", "aA1", "aA2", "aB0", "aB1", "aB2"]
+
+
+def clash(a, b):
+    if a["names"] & b["names"]:
+        for n, m in a["w"]:
+            if any(n == k and m & x for k, x in b["r"] + b["w"]):
+                return not (a["sum"] and b["sum"])
+        for n, m in a["r"]:
+            if any(n == k and m & x for k, x in b["w"]):
+                return True
+    return a["q"] != b["q"] and bool(a["banks"] & b["banks"])
 
 
 def schedule(g, T, ops):
     queues = {"V": g.vector, "S": g.scalar, "P": g.tensor, "G": g, "Y": g.sync}
     known = {q: {} for q in queues}
-    writer, readers, pos = {}, {}, {q: 0 for q in queues}
+    pos = {q: 0 for q in queues}
     for n, o in enumerate(ops):
         q = o["q"]
-        deps = set()
-        for k in o["r"]:
-            if k in writer:
-                deps.add(writer[k])
-        for k in o["w"]:
-            if k in writer:
-                deps.add(writer[k])
-            deps.update(readers.get(k, []))
         o["waits"] = []
         if q is not None:
-            for d in sorted(deps, reverse=True):
+            for d in range(n - 1, -1, -1):
                 e = ops[d]
-                if e["tok"] is None or known[q].get(e["tok"], 0) >= e["at"]:
+                if e["tok"] is None or known[q].get(e["tok"], 0) >= e["at"] or not clash(e, o):
                     continue
                 o["waits"].append(d)
                 e["inc"] = True
@@ -80,11 +95,6 @@ def schedule(g, T, ops):
         o["clock"] = dict(known[q]) if q is not None else {}
         if o["tok"] is not None:
             o["clock"][o["tok"]] = o["at"]
-        for k in o["r"]:
-            readers.setdefault(k, []).append(n)
-        for k in o["w"]:
-            writer[k] = n
-            readers[k] = []
     count = {q: 0 for q in queues}
     for o in ops:
         if o["q"] is None:
@@ -108,290 +118,348 @@ def rank_program(g, core, T, topo):
     ops = []
     V, S = g.vector, g.scalar
 
-    def op(q, f, r, w, sem=None, loose=False, val=16):
-        ops.append({"q": q, "f": f, "r": list(r), "w": list(w), "sem": sem, "loose": loose, "val": val})
+    def v(name, lo=0, hi=None, step=1):
+        hi = SCRATCH[name][1][1] if hi is None else hi
+        mask = sum(1 << c for c in range(lo, hi, step)) if step > 1 else (1 << hi) - (1 << lo)
+        return (T[name][:, lo:hi:step] if step > 1 else T[name][:, lo:hi], [(name, mask)], [])
 
-    def ts(out, in0, s1, s2, op0, op1, r, w):
+    def by(win, off, words=False):
+        ap = win[0].bitcast(dt.uint32) if words else win[0]
+        return (ap.indirect(off[0]), win[1], off[1])
+
+    def raw(x, d):
+        return (x[0].bitcast(d), x[1], x[2])
+
+    def bank(b, lo=0, hi=C):
+        return v("ps", 512 * b + lo, 512 * b + hi)
+
+    def op(q, f, outs, ins, sem=None, loose=False, val=16, adds=False):
+        ins = [x for x in ins if isinstance(x, tuple)]
+        w = [k for x in outs for k in x[1]]
+        r = [k for x in ins for k in x[1]] + [k for x in outs + ins for k in x[2]]
+        banks = {b for n, m in r + w if n == "ps" for b in range(8) if m >> (512 * b) & ((1 << 512) - 1)}
+        ops.append({"q": q, "f": f, "r": r, "w": w, "sem": sem, "loose": loose, "val": val, "banks": banks, "sum": adds,
+                    "names": {n for n, m in r + w}})
+
+    def a_(x):
+        return x[0] if isinstance(x, tuple) else x
+
+    def ts(out, in0, s1, op0, s2=None, op1=None):
         if op1 is None:
-            op("V", lambda: V.tensor_scalar(out, in0, s1, None, op0), r, w)
+            op("V", lambda: V.tensor_scalar(out[0], in0[0], a_(s1), None, op0), [out], [in0, s1])
         else:
-            op("V", lambda: V.tensor_scalar(out, in0, s1, s2, op0, op1), r, w)
+            op("V", lambda: V.tensor_scalar(out[0], in0[0], a_(s1), a_(s2), op0, op1), [out], [in0, s1, s2])
 
-    def tt(out, in0, in1, o, r, w):
-        op("V", lambda: V.tensor_tensor(out, in0, in1, o), r, w)
+    def tt(out, in0, in1, o):
+        op("V", lambda: V.tensor_tensor(out[0], in0[0], in1[0], o), [out], [in0, in1])
 
-    def cp(out, in_, r, w):
-        op("V", lambda: V.tensor_copy(out, in_), r, w)
+    def cp(out, in_):
+        op("V", lambda: V.tensor_copy(out[0], in_[0]), [out], [in_])
 
-    def scan(out, d0, d1, init, op0, op1, r, w):
-        op("V", lambda: V.tensor_tensor_scan(out, d0, d1, init, op0, op1), r, w)
+    def scan(out, d0, d1, init, op0, op1):
+        op("V", lambda: V.tensor_tensor_scan(out[0], d0[0], d1[0], a_(init), op0, op1), [out], [d0, d1, init])
 
-    def ms(ap, v, w):
-        op("V", lambda: V.memset(ap, v), [], w)
+    def ms(out, x):
+        op("V", lambda: V.memset(out[0], x), [out], [])
 
-    def qz(codes, scales, tile, r, w):
-        op("V", lambda: V.quantize_mx(codes, scales, tile), r, w)
+    def qz(codes, scales, tile):
+        op("V", lambda: V.quantize_mx(codes[0], scales[0], tile[0]), [codes, scales], [tile])
 
-    def act(out, in_, func, r, w, bias=0.0, scale=1.0, acc=None):
+    def act(out, in_, func, bias=0.0, scale=1.0, acc=None):
         if acc is None:
-            op("S", lambda: S.activation(out, in_, func, bias=bias, scale=scale), r, w)
+            op("S", lambda: S.activation(out[0], in_[0], func, bias=a_(bias), scale=scale), [out], [in_, bias])
         else:
-            op("S", lambda: S.activation(out, in_, func, bias=bias, scale=scale, accum_out=acc), r, w)
+            op("S", lambda: S.activation(out[0], in_[0], func, bias=a_(bias), scale=scale, accum_out=acc[0]), [out, acc], [in_, bias])
 
-    def acp(out, in_, r, w, scale=None):
-        if scale is None:
-            op("S", lambda: S.activation(out, in_, AF.Copy), r, w)
+    def acp(out, in_):
+        op("S", lambda: S.activation(out[0], in_[0], AF.Copy), [out], [in_])
+
+    def times(e, out, in_, x):
+        if e == "V":
+            ts(out, in_, x, A.mult)
         else:
-            op("S", lambda: S.activation(out, in_, AF.Copy, scale=scale), r, w)
+            op("S", lambda: S.activation(out[0], in_[0], AF.Copy, scale=x), [out], [in_])
 
-    def mm(bank, n, lq, lsc, rq, rsc, r):
-        op("P", lambda: g.tensor.matmul_mx(T.ps[:, 512 * bank:512 * bank + n], lq, lsc, rq, rsc, True, True), r, ["ps%d" % bank])
+    def mm(b, left, lo, right, r0, r1, start=True, stop=True):
+        out, a = bank(b, 0, r1 - r0), [v(n, lo, lo + 128) for n in left] + [v(n, r0, r1) for n in right]
+        op("P", lambda: g.tensor.matmul_mx(out[0], a[0][0], a[1][0], a[2][0], a[3][0], start, stop), [out], a, adds=not (start and stop))
 
-    def iota(out, pattern, base, cm, w, real=False):
+    def iota(out, pattern, base, cm, real=False):
         if real:
-            op("G", lambda: g.iota(out, pattern, base, cm, allow_small_or_imprecise_dtypes=True), [], w)
+            op("G", lambda: g.iota(out[0], pattern, base, cm, allow_small_or_imprecise_dtypes=True), [out], [])
         else:
-            op("G", lambda: g.iota(out, pattern, base, cm), [], w)
+            op("G", lambda: g.iota(out[0], pattern, base, cm), [out], [])
+
+    def keep(out, in_, pattern, base, cm, how):
+        op("G", lambda: g.affine_select(out[0], in_[0], pattern, how, 0.0, base, cm), [out], [in_])
 
     sent = [0]
 
-    def send(peer, out, in_, sem, r):
+    def send(peer, out, in_, sem):
         rid, pid, _se = topo.addr(peer)
         sent[0] += len(topo.engines(core, peer))
-        op("G", lambda: g.remote_dma(out, in_, T.sem[sem], T.sem.sent, pid, rid, topo.mask(core, peer)), r, [], loose=True)
+        op("G", lambda: g.remote_dma(out[0], in_[0], T.sem[sem], T.sem.sent, pid, rid, topo.mask(core, peer)), [], [in_], loose=True)
 
-    def bank(b, lo=0, hi=C):
-        return T.ps[:, 512 * b + lo:512 * b + hi]
+    def load(q, out, src, sem, after=()):
+        e = g.sync if q == "Y" else S
+        op(q, lambda: e.dma_start(out[0], src), [out], list(after), sem=sem)
 
-    op("S", lambda: S.dma_start(T.ub[:], T.u[:]), [], ["ub"], sem="lu")
-    op("Y", lambda: g.sync.dma_start(T.tt0[:], T.x[:]), [], ["T0"], sem="lx")
-    op("Y", lambda: g.sync.dma_start(T.qw[:].bitcast(dt.uint8), T.wc[:]), ["T0"], ["qw"], sem="lwc")
-    op("Y", lambda: g.sync.dma_start(T.sw[:], T.ws[:]), [], ["sw"], sem="lws")
-    op("Y", lambda: g.sync.dma_start(T.vb[:], T.v[:]), [], ["vb"], sem="lv")
-
-    iota(T.i16[:], [[1, 16]], 128, -1, ["i16"])
-    iota(T.ipm[:], [[0, Q]], 0, 1, ["ipm"])
-    iota(T.iou[:], [[1, 2], [16, 8]], 0, 0, ["iou"])
-    iota(T.iid[:], [[1, 128]], 0, -1, ["iid"])
-    iota(T.nb[:], [[16, Q]], 16, 0, ["nb"], real=True)
-    iota(T.i24[:, 0:EV], [[16, EV]], 0, 0, ["i24a"])
-    iota(T.i24[:, EV:EQ], [[16, ES]], 16 * (Q - ES), 0, ["i24b"])
-    iota(T.i24[:, EQ:Q], [[16, Q - EQ]], 16 * EV, 0, ["i24c"])
-    ms(T.eb[:], 0.0, ["eb0", "eb1", "eb2", "eb3"])
-    ts(T.r16[:], T.i16[:], 15, None, A.bitwise_and, None, ["i16"], ["r16"])
-    ts(T.rpm[:], T.ipm[:], 15, None, A.bitwise_and, None, ["ipm"], ["rpm"])
-    cp(T.ou[:], T.iou[:], ["iou"], ["ou"])
-    ts(T.dm16[:], T.r16[:], 0, None, A.is_equal, None, ["r16"], ["dm16"])
-    cp(T.pm[:], T.rpm[:], ["rpm"], ["pm"])
-    ts(T.kp16[:], T.r16[:], 0, None, A.not_equal, None, ["r16"], ["kp16"])
-    ts(T.t16[:], T.r16[:], 1.0, BIG, A.is_equal, A.mult, ["r16"], ["t16"])
-    ms(T.tab[:, M:C], 0.0, ["tab1"])
-    tt(T.c16[:], T.t16[:], T.kp16[:], A.max, ["t16", "kp16"], ["c16"])
-    for b in range(4):
-        ts(T.eb[:, 512 * b + b:512 * (b + 1):4], T.iid[:], 0, None, A.is_equal, None, ["iid"], ["eb%d" % b])
-    ms(T.tab[:, 0:M], 1.0, ["tab0"])
-    ms(T.tab[:, C:C + M], 1.0, ["tab2"])
-    acp(T.dm[:], T.dm16[:].indirect(T.pm[:]), ["dm16", "pm"], ["dm"])
-    acp(T.kp[:], T.kp16[:].indirect(T.pm[:]), ["kp16", "pm"], ["kp"])
-    acp(T.cm[:], T.c16[:].indirect(T.pm[:]), ["c16", "pm"], ["cm"])
-    ts(T.inv[:, 0:1], T.dm16[:, 15:16], 1.0 - 1.0 / BIG, 1.0 / BIG, A.mult, A.add, ["dm16"], ["inv0"])
-    ts(T.inv[:, 2:3], T.dm16[:, 15:16], BIG - 1.0, -BIG, A.mult, A.add, ["dm16"], ["inv2"])
-    ms(T.b0[:], 1.0, ["b0", "b0b"])
-    ms(T.a0[:, 0:3 * NS:3], 0.0, ["a00"])
-    ms(T.a0[:, 1:3 * NS:3], 1.0, ["a01"])
-    ms(T.a0[:, 2:3 * NS:3], -1.0, ["a02"])
-    ms(T.a1[:], 0.0, ["a1c"] + ["a1_%d" % i for i in range(2 * NS)])
-    ms(T.b0[:, 0:4 * Q:4], 0.0, ["b0"])
-    tt(T.x24[:], T.i24[:], T.rpm[:], A.add, ["i24a", "i24b", "i24c", "rpm"], ["x24"])
-    qz(T.qu[:], T.su[:], T.ub[:], ["ub"], ["qu"])
-    cp(T.qp[:].bitcast(dt.uint32), T.qu[:].bitcast(dt.uint32).indirect(T.ou[:]), ["qu", "ou"], ["qp"])
-    acp(T.sp[:], T.su[:].indirect(T.ou[:]), ["qu", "ou"], ["sp"])
-    qz(T.qt0[:], T.sq0[:], T.tt0[:], ["T0"], ["q0"])
-    qz(T.qe[:], T.se[:], T.eb[:], ["eb0", "eb1", "eb2", "eb3"], ["qe"])
-
-    def plane0(b):
-        acp(T.win0[:, 2 * C * b:2 * C * b + C], T.tt0[:, b:4 * C:4], ["T0"], ["W0_%d" % b], scale=64.0)
-
-    plane0(0)
-    plane0(1)
-
-    c0, h, e0 = 16 * NV, C // 2, 16 * EQ
-    for t in range(R):
-        peer = T.cores[rank ^ STEP[t]]
-        ne = len(topo.engines(peer, core))
-        win, nxt, tile = T["win%d" % t], T["win%d" % (t + 1)], T["tt%d" % (t + 1)]
-        qt, sq = T["qt%d" % t], T["sq%d" % t]
-        lq, ls, rk, lr = T["lq%d" % t], T["ls%d" % t], T["rk%d" % t], T["lr%d" % t]
-        kq, kn = "q%d" % t, "T%d" % (t + 1)
-        le, ll = "le%d" % t, "ll%d" % t
-        send(peer, lq[:].bitcast(dt.uint8), qt[:].bitcast(dt.uint8), "ac%d" % t, [kq])
-        send(peer, ls[:], sq[:], "ac%d" % t, [kq])
-        op(None, None, [], ["lq%d" % t], sem="ac%d" % t, val=2 * ne)
-        op(None, None, [], [le], sem="ae%d" % t, val=ne)
-        op(None, None, [], [ll], sem="al%d" % t, val=ne)
-        if t == 0:
-            iota(T.vtab[:], [[1, 2 * C]], 1, 0, ["vtab"], real=True)
-            iota(T.htab[:], [[0, 2], [1, C]], 0, 0, ["htab"], real=True)
-        if t == 1:
-            qz(T.qv[:], T.sv[:], T.vb[:], ["vb"], ["qv"])
-        mm(0, C, T.qp[:, 0:128], T.sp[:, 0:128], qt[:], sq[:], ["qp", "sp", kq])
-        mm(2, C, T.qp[:, 128:256], T.sp[:, 128:256], qt[:], sq[:], ["qp", "sp", kq])
-        mm(1, C, T.qp[:, 0:128], T.sp[:, 0:128], qt[:], sq[:], ["qp", "sp", kq])
-        for b in range(4):
-            mm(4 + b, C, T.qe[:, 128 * b:128 * (b + 1)], T.se[:, 128 * b:128 * (b + 1)], lq[:], ls[:], ["qe", "lq%d" % t])
-        tt(T.mk[:, c0:C], bank(0, c0, C), T.dm[:, c0:C], A.mult, ["ps0", "dm"], ["mk2"])
-        tt(T.mk[:, 0:c0], bank(0, 0, c0), T.dm[:, 0:c0], A.mult, ["ps0", "dm"], ["mk1"])
-        scan(T.hold[:, c0:C], T.kp[:, c0:C], T.mk[:, c0:C], 0.0, A.mult, A.add, ["kp", "mk2"], ["h2"])
-        scan(T.hold[:, 0:c0], T.kp[:, 0:c0], T.mk[:, 0:c0], 0.0, A.mult, A.add, ["kp", "mk1"], ["h1"])
-        act(T.cf[:], bank(2), AF.Sign, ["ps2"], ["cf"])
-
-        def sign(i):
-            m = NV + i
-            act(T.fs[:, i * C:(i + 1) * C], bank(1), AF.Sign, ["ps1", "h2"], ["fs%da" % i, "fs%db" % i],
-                bias=T.hold[:, 16 * m + 15:16 * m + 16], scale=-1.0)
-
-        def sums(i):
-            e = 16 * (NV + i + 1)
-            a = T.fs[:, i * C:i * C + e]
-            act(a, a, AF.Relu, ["fs%da" % i], ["fs%da" % i, "a1_%d" % (2 * i)], acc=T.a1[:, 3 * i + 1:3 * i + 2])
-            if e < C:
-                a = T.fs[:, i * C + e:(i + 1) * C]
-                act(a, a, AF.Relu, ["fs%db" % i], ["fs%db" % i, "a1_%d" % (2 * i + 1)], scale=-1.0, acc=T.a1[:, 3 * i + 2:3 * i + 3])
-
-        for i in range(NS - 1, -1, -1):
-            sign(i)
-            if i < NS - 1:
-                sums(i + 1)
-        sums(0)
-        act(T.cf[:], T.cf[:], AF.Relu, ["cf"], ["cf", "st0"], acc=T.st[:, 0:1])
-        act(T.st[:, 1:2], T.st[:, 0:1], AF.Relu, ["st0"], ["st1"], bias=float(M), scale=-1.0)
-
-        def compare(m):
-            e = 16 * (m + 1)
-            s = T.hold[:, 16 * m + 15:16 * m + 16]
-            ts(T.fv[:, m * C:m * C + e], bank(0, 0, e), s, None, A.is_ge, None, ["ps0", "h1"], ["fv%da" % m])
-            ts(T.fv[:, m * C + e:(m + 1) * C], bank(0, e, C), s, None, A.is_gt, None, ["ps0", "h1"], ["fv%db" % m])
-
-        def total(m):
-            scan(T.zv[:, m * h:(m + 1) * h], T.fv[:, m * C:m * C + h], T.fv[:, m * C + h:(m + 1) * C], T.ci[:, m:m + 1],
-                 A.add, A.add, ["fv%da" % m, "fv%db" % m, "ci"], ["zv%d" % m])
-
-        def fold(i0, i1, key):
-            scan(T.ao[:, 3 * i0:3 * i1], T.a0[:, 3 * i0:3 * i1], T.a1[:, 3 * i0:3 * i1], 0.0, A.mult, A.add,
-                 ["a00", "a01", "a02", "a1c"] + ["a1_%d" % i for i in range(2 * i0, 2 * i1)], [key])
-
-        def places(at, m0, m1, key):
-            ts(rk[:, at:at + m1 - m0], T.zv[:, (m0 + 1) * h - 1:m1 * h:h], float(h), None, A.add, None,
-               ["zv%d" % m for m in range(m0, m1)], [key])
-
-        tt(T.eq[:, c0:C], bank(0, c0, C), T.hold[:, c0:C], A.is_equal, ["ps0", "h2"], ["eq2"])
-        tt(T.eq[:, 0:c0], bank(0, 0, c0), T.hold[:, 0:c0], A.is_equal, ["ps0", "h1"], ["eq1"])
-        compare(0)
-        scan(T.cr[:], T.kp[:], T.eq[:], 0.0, A.mult, A.add, ["kp", "eq1", "eq2"], ["cr"])
-        compare(1)
-        ts(T.ci[:, 0:NV], T.cr[:, 15:c0:16], -1.0, -float(h), A.mult, A.add, ["cr"], ["ci"])
-        tt(T.a1[:, 0:3 * NS:3], T.cr[:, c0 + 15:C:16], T.nb[:, NV:Q], A.subtract, ["cr", "nb"], ["a1c"])
-        compare(2)
-        total(0)
-        total(1)
-        kr = ["rk%d%s" % (t, n) for n in "abcd"]
-        for m in range(3, NV):
-            compare(m)
-            if m == EV + 1:
-                places(0, 0, EV, kr[0])
-                cp(rk[:, EV:EQ], T.ao[:, 3 * (NS - ES) + 2:3 * NS:3], ["aoe"], [kr[1]])
-                send(peer, lr[:, 0:EQ], rk[:, 0:EQ], "ae%d" % t, kr[0:2])
-            total(m - 1)
-            if m == EV:
-                fold(NS - ES, NS, "aoe")
-        total(NV - 1)
-        fold(0, NS - ES, "aol")
-        places(EQ, EV, NV, kr[2])
-        cp(rk[:, EQ + NV - EV:Q], T.ao[:, 2:3 * (NS - ES):3], ["aol"], [kr[3]])
-        send(peer, lr[:, EQ:Q], rk[:, EQ:Q], "al%d" % t, kr[2:4])
-
-        r = T.st[:, 1:2]
-        ts(T.z16[:, 0:EQ], rk[:, 0:EQ], r, None, A.add, None, kr[0:2] + ["st1"], ["ze"])
-        ts(T.z16[:, EQ:Q], rk[:, EQ:Q], r, None, A.add, None, kr[2:4] + ["st1"], ["zl"])
-        ts(T.lo[:], rk[:], r, float(M), A.add, A.is_lt, kr + ["st1"], ["lo"])
-        ts(T.hi[:], rk[:], r, float(C), A.add, A.is_ge, kr + ["st1"], ["hi"])
-        ts(T.b1[:, 2:4 * Q:4], rk[:], -1.0, -1.0, A.mult, A.add, kr, ["b12"])
-        tt(T.b0[:, 3:4 * Q:4], T.lo[:], T.hi[:], A.add, ["lo", "hi"], ["b0b"])
-        cp(T.b1[:, 3:4 * Q:4], rk[:], kr, ["b13"])
-        ts(T.v1[:], T.b0[:, 3:4 * Q:4], float(C), None, A.mult, None, ["b0b"], ["v1"])
-        tabs = ["tab0", "tab1", "tab2"]
-
-        def unpack(b):
-            acp(win[:, 2 * C * b + C:2 * C * (b + 1)], bank(4 + b), ["ps%d" % (4 + b)], ["D%d_%d" % (t, b)], scale=64.0)
-
-        acp(T.nk[:, 0:e0], T.tab[:].indirect(T.z16[:, 0:EQ]), tabs + ["ze"], ["nke"])
-        acp(T.nk[:, e0:C], T.tab[:].indirect(T.z16[:, EQ:Q]), tabs + ["zl"], ["nkl"])
-        unpack(0)
-        unpack(1)
-
-        cp(T.np1[:].indirect(lr[:, 0:EQ]), T.nk[:, 0:e0], ["nke", le], ["np1"])
-        tt(T.v2[:], T.v1[:], T.x24[:], A.add, ["v1", "x24"], ["v2"])
-        ts(T.st[:, 2:3], r, -float(M), T.inv[:, 2:3], A.add, A.mult, ["st1", "inv2"], ["st2"])
-        cp(T.v16[:], T.v2[:], ["v2"], ["v16"])
-        cp(T.np1[:].indirect(lr[:, EQ:Q]), T.nk[:, e0:C], ["nkl", ll], ["np1"])
-        scan(T.tc[:], T.np1[:], T.np1[:], 0.0, A.add, A.max, ["np1"], ["tc"])
-        cp(T.tx[:, 0:h], T.tc[:].indirect(lr[:, 0:Q // 2]), ["tc", le, ll], ["tx0"])
-        acp(T.tx[:, h:C], T.tc[:].indirect(lr[:, Q // 2:Q]), ["tc", le, ll], ["tx1"])
-        acp(T.val[:], T.vtab[:].indirect(T.v16[:]), ["vtab", "v16"], ["val"])
-        unpack(2)
-        unpack(3)
-        if t == 0:
-            plane0(2)
-            plane0(3)
-        scan(T.td[:], T.cm[:], T.tx[:], 0.0, A.mult, A.max, ["cm", "tx0", "tx1"], ["td"])
-        ts(T.b1[:, 0:4 * Q:4], T.td[:, 15:C:16], T.inv[:, 0:1], None, A.mult, None, ["td", "inv0"], ["b10"])
-        ts(T.b1[:, 1:4 * Q:4], T.td[:, 15:C:16], T.st[:, 2:3], float(L), A.is_gt, A.mult, ["td", "st2"], ["b11"])
-        scan(T.bo[:], T.b0[:], T.b1[:], 0.0, A.mult, A.add, ["b0", "b0b", "b10", "b11", "b12", "b13"], ["bo"])
-        cp(T.pl[:], T.bo[:, 3:4 * Q:4], ["bo"], ["pl"])
-        cp(T.idx[:].indirect(T.pl[:]), T.val[:], ["val", "pl"], ["idx"])
-        scan(T.idd[:], T.cm[:], T.idx[:], 0.0, A.mult, A.max, ["cm", "idx"], ["idd"])
-        ts(T.off[:], T.idd[:, 15:C:16], T.inv[:, 0:1], -1.0, A.mult, A.add, ["idd", "inv0"], ["off"])
-        for b in range(4):
-            src = win[:, 2 * C * b:2 * C * (b + 1)].indirect(T.off[:])
-            kw = ["W%d_%d" % (t, b), "D%d_%d" % (t, b), "off"]
-            if b < 2:
-                acp(T.ft[:, b:4 * C:4], src, kw, ["ft%d" % b], scale=0.015625)
-            else:
-                ts(T.ft[:, b:4 * C:4], src, 0.015625, None, A.mult, None, kw, ["ft%d" % b])
-        kf = ["ft%d" % b for b in range(4)]
-        qz(T.qf[:], T.sf[:], T.ft[:], kf, ["qf"])
-        for b in range(4):
-            mm(4 + b, C, T.qw[:, 128 * b:128 * (b + 1)], T.sw[:, 128 * b:128 * (b + 1)], T.qf[:], T.sf[:], ["qw", "sw", "qf"])
-        for b in range(2):
-            acp(T.f64[:, C * b:C * (b + 1)], T.ft[:, b:4 * C:4], ["ft%d" % b], ["f64%d" % b], scale=64.0)
-        for b in range(2, 4):
-            ts(T.f64[:, C * b:C * (b + 1)], T.ft[:, b:4 * C:4], 64.0, None, A.mult, None, ["ft%d" % b], ["f64%d" % b])
-        for b in range(4):
-            tt(nxt[:, 2 * C * b:2 * C * b + C], bank(4 + b), T.f64[:, C * b:C * (b + 1)], A.add,
-               ["ps%d" % (4 + b), "f64%d" % b], ["W%d_%d" % (t + 1, b)])
-        for b in range(3):
-            acp(tile[:, b:4 * C:4], nxt[:, 2 * C * b:2 * C * b + C], ["W%d_%d" % (t + 1, b)], [kn + "_%d" % b], scale=0.015625)
-        ts(tile[:, 3:4 * C:4], nxt[:, 6 * C:7 * C], 0.015625, None, A.mult, None, ["W%d_3" % (t + 1)], [kn + "_3"])
-        qz(T["qt%d" % (t + 1)][:], T["sq%d" % (t + 1)][:], tile[:], [kn + "_%d" % b for b in range(4)], ["q%d" % (t + 1)])
-
-    qt, sq, kq = T["qt%d" % R], T["sq%d" % R], "q%d" % R
-    acp(T.hrow[:], T.htab[:].indirect(T.off[:]), ["htab", "off"], ["hrow"])
-    mm(0, h, T.qv[:], T.sv[:], qt[:, 0:h], sq[:, 0:h], ["qv", kq])
-    mm(1, h, T.qv[:], T.sv[:], qt[:, h:C], sq[:, h:C], ["qv", kq])
-    cp(T.ys[:, 0:h], bank(0, 0, h), ["ps0"], ["ys0"])
-    acp(T.ys[:, h:C], bank(1, 0, h), ["ps1"], ["ys1"])
     stores = {"sto": 0, "sty": 0}
 
     def store(q, sem, out, in_, r):
         stores[sem] += 16
         e = g.sync if q == "Y" else S
-        op(q, lambda: e.dma_start(out, in_).then_inc(T.sem[sem], 16), r, [], loose=True)
+        op(q, lambda: e.dma_start(out, in_).then_inc(T.sem[sem], 16), [], [r], loose=True)
 
-    store("Y", "sto", T.oc[:], qt[:].bitcast(dt.uint8), [kq])
-    for k in range(4):
-        store("Y", "sto", T.osc[4 * k:4 * k + 4, :], sq[32 * k:32 * k + 4, :], [kq])
-    store("Y", "sto", T.ot[:], T.hrow[0:128:16, :], ["hrow"])
-    store("S", "sty", T.y[:], T.ys[:], ["ys0", "ys1"])
+    load("S", v("ub"), T.u[:], "lu")
+    load("Y", v("tt0", 0, 4 * H), T.x[:, 0:4 * H], "lxA")
+    load("Y", v("tt0", 4 * H), T.x[:, 4 * H:4 * C], "lxB")
+    load("Y", raw(v("qw"), dt.uint8), T.wc[:], "lwc", [v("tt0")])
+    load("Y", v("sw"), T.ws[:], "lws")
+    load("Y", v("vb"), T.v[:], "lv")
+
+    iota(v("i16"), [[1, 16]], 128, -1)
+    iota(v("ipm"), [[0, Q]], 0, 1)
+    iota(v("iou"), [[1, 2], [16, 8]], 0, 0)
+    iota(v("i24"), [[16, Q]], 0, 0)
+    ms(v("one"), 1.0)
+    for b in range(2):
+        keep(v("eb", 528 * b, 528 * b + 514), v("one"), [[1, 514]], -2 - b, -4, A.is_equal)
+    keep(v("gb"), v("one", 0, 512), [[16, 8], [0, 64]], 15, -1, A.is_ge)
+    keep(v("gs"), v("gb"), [[-16, 8], [0, 64]], 0, 1, A.is_ge)
+    ms(v("fl", 4 * AT[-2]), 0.0)
+    ts(v("r16"), v("i16"), 15, A.bitwise_and)
+    ts(v("rpm"), v("ipm"), 15, A.bitwise_and)
+    ms(v("n16", 0, 1), -FAR)
+    ms(v("b0"), 1.0)
+    ts(v("dm16"), v("r16"), 0, A.is_equal)
+    cp(v("pm"), v("rpm"))
+    ts(v("kp16"), v("r16"), 0, A.not_equal)
+    ts(v("t16"), v("r16"), 1.0, A.is_equal, BIG, A.mult)
+    ts(v("l16"), v("r16"), 15.0, A.is_equal, -LOCK, A.mult)
+    ts(v("m16"), v("dm16"), 2 * FAR, A.mult, -FAR, A.add)
+    ts(v("n16", 1), v("dm16", 1), -2 * FAR, A.mult, FAR, A.add)
+    ts(v("e16"), v("dm16"), BIG, A.mult)
+    cp(v("ou"), v("iou"))
+    tt(v("c16"), v("t16"), v("kp16"), A.max)
+    acp(v("am"), by(v("m16"), v("pm")))
+    acp(v("km"), by(v("n16"), v("pm")))
+    acp(v("kp"), by(v("kp16"), v("pm")))
+    tt(v("a16"), v("e16"), v("l16"), A.add)
+    last = v("dm16", 15, 16)
+    ts(v("inv", 0, 1), last, 1.0 - 1.0 / BIG, A.mult, 1.0 / BIG, A.add)
+    ts(v("inv", 1, 2), v("dm16", 0, 1), LOCK, A.mult, H - BIG, A.add)
+    ts(v("inv", 2, 3), last, BIG - 1.0, A.mult, -BIG, A.add)
+    tt(v("x24"), v("i24"), v("rpm"), A.add)
+    tt(v("ca"), v("rpm"), v("i24"), A.subtract)
+    ms(v("b0", 0, 4 * Q, 4), 0.0)
+    for a in range(len(QUADS) - 1):
+        ms(v("fl", 4 * (AT[a + 1] - 48), 4 * AT[a + 1]), 0.0)
+    ts(v("ca"), v("ca"), float(H - 15), A.add)
+    qz(v("qu"), v("su"), v("ub"))
+    qz(v("qc", AT[-2]), v("sc", AT[-2]), v("fl", 4 * AT[-2]))
+    cp(raw(v("qp"), dt.uint32), by(v("qu"), v("ou"), True))
+    acp(v("sp"), by(v("su"), v("ou")))
+    acp(v("ad"), by(v("a16"), v("pm")))
+    acp(v("cm"), by(v("c16"), v("pm")))
+    for b in range(4):
+        lo = 528 * (b % 2) + 2 - b // 2 * 2
+        qz(v("qe", 128 * b, 128 * (b + 1)), v("se", 128 * b, 128 * (b + 1)), v("eb", lo, lo + 512))
+
+    def slot(m, lo, hi, step=4, first=0):
+        a = [m in rows for rows in QUADS].index(True)
+        at = 4 * AT[a] + QUADS[a].index(m)
+        return v("fl", at + 4 * lo + first, at + 4 * hi, step)
+
+    def ends(name, rows, w=1):
+        step = rows[1] - rows[0] if len(rows) > 1 else 1
+        return v(name, w * rows[0] + w - 1, w * rows[-1] + w, w * step)
+
+    def score(m):
+        return v("hold", 16 * m + 15, 16 * m + 16)
+
+    up, sums, gone = ("qp", "sp"), ("qc", "sc"), v("st", 1, 2)
+
+    def layer(w, t):
+        lo = H if "B" in w else 0
+        hi = lo + H
+        if w[:2] == "qf":
+            qz(v("qf", lo, hi), v("sf", lo, hi), v("ft", 4 * lo, 4 * hi))
+            return
+        if w[0] == "w":
+            for b in range(4):
+                mm(b if lo else 4 + b, ("qw", "sw"), 128 * b, ("qf", "sf"), lo, hi)
+            return
+        b = int(w[2])
+        part, big = v("ft", 4 * lo + b, 4 * hi, 4), v("f64", C * b + lo, C * b + hi)
+        new = v("win%d" % t, 2 * C * b + lo, 2 * C * b + hi)
+        if w[0] == "g":
+            times(w[3], part, by(v("win%d" % (t - 1), 2 * C * b, 2 * C * (b + 1)), v("off", lo // 16, hi // 16)), 0.015625)
+        elif w[0] == "f":
+            times(w[3], big, part, 64.0)
+        elif w[0] == "t":
+            tt(new, bank(b if lo else 4 + b, 0, H), big, A.add)
+        else:
+            times(w[3], v("tt%d" % t, 4 * lo + b, 4 * hi, 4), new, 0.015625)
+
+    def leave(w):
+        qt, sq = "qt%d" % R, "sq%d" % R
+        if w == "hrow":
+            acp(v("hrow"), by(v("htab"), v("off")))
+            store("S", "sty", T.ot[:], T.hrow[0:128:16, :], v("hrow"))
+            return
+        lo = H if w in ("yB", "yb") else 0
+        hi = lo + H
+        if w in ("ya", "yb"):
+            cp(v("ys", lo, hi), bank(lo // H + 4, 0, H))
+            store("Y", "sto", T.y[:, lo:hi], T.ys[:, lo:hi], v("ys", lo, hi))
+            return
+        store("Y", "sto", T.oc[:, 4 * lo:4 * hi], T[qt][:, lo:hi].bitcast(dt.uint8), v(qt, lo, hi))
+        mm(lo // H + 4, ("qv", "sv"), 0, (qt, sq), lo, hi)
+        if lo:
+            for k in range(4):
+                store("S", "sty", T.osc[4 * k:4 * k + 4, :], T[sq][32 * k:32 * k + 4, :], v(sq))
+
+    def count(w, t):
+        peer = T.cores[rank ^ STEP[t]]
+        state, rk = ("qt%d" % t, "sq%d" % t), "rk%d" % t
+        half = w[-1]
+        lo = H if half == "B" else 0
+        hi, rows = lo + H, list(range(lo // 16, lo // 16 + K))
+        scores = bank(0, H) if lo else bank(4, 0, H)
+        if w == "send":
+            ne = len(topo.engines(peer, core))
+            lq, ls = v("lq%d" % t), v("ls%d" % t)
+            send(peer, raw(lq, dt.uint8), raw(v(state[0]), dt.uint8), "ac%d" % t)
+            send(peer, ls, v(state[1]), "ac%d" % t)
+            op(None, None, [lq, ls], [], sem="ac%d" % t, val=2 * ne)
+            for h in "AB":
+                op(None, None, [v("l%s%d" % (h, t))], [], sem="a%s%d" % (h, t), val=ne)
+            if t == 0:
+                for a, b, x in ((0, M, 1), (M, C, 0), (C, C + M, 1)):
+                    iota(v("tab", a, b), [[0, b - a]], x, 0, real=True)
+                iota(v("vtab"), [[1, 2 * C]], 1, 0, real=True)
+            if t == 1:
+                iota(v("htab"), [[0, 2], [1, C]], 0, 0, real=True)
+        elif w == "pA":
+            mm(4, up, 0, state, 0, H)
+            mm(5, up, 0, state, 0, H)
+        elif w == "pF":
+            for b, c in ((0, 0), (2, 128), (1, 0)):
+                mm(b, up, c, state, 0, C)
+        elif w[:2] == "mk":
+            tt(v("mk", lo, hi), scores, v("am", lo, hi), A.min)
+        elif w[:2] == "hd":
+            scan(v("hold", lo, hi), v("km", lo, hi), v("mk", lo, hi), 0.0, A.min, A.max)
+        elif w[:3] == "own":
+            tt(slot(lo // 16, lo, hi), scores, v("hold", lo, hi), A.is_le)
+        elif w[:2] == "cr":
+            scan(v("cr", lo, hi), v("kp", lo, hi), slot(lo // 16, lo, hi), 0.0, A.mult, A.add)
+        elif w[:2] == "ci":
+            tt(ends("ci", rows), ends("cr", rows, 16), ends("ca", rows), A.add)
+        elif w == "n1":
+            act(v("cf"), bank(2), AF.Sign)
+        elif w == "n2":
+            act(v("cf"), v("cf"), AF.Relu, acc=v("st", 0, 1))
+        elif w == "n3":
+            act(gone, v("st", 0, 1), AF.Relu, bias=float(M), scale=-1.0)
+        elif w == "f0":
+            cp(ends("zv", [0], W), v("ci", 0, 1))
+        elif w[0] == "f":
+            for run in RUNS[half]:
+                tt(ends("zv", run, W), ends("acc", run), ends("ci", run), A.add)
+        elif w[0] == "x":
+            ts(ends("ad", rows, 16), ends("zv", rows, W), -1.0, A.mult, v("a16", 15, 16), A.add)
+        elif w[0] == "d":
+            scan(v("cd", lo, hi), bank(3, H - 128, C - 128) if lo else bank(6, 0, H), v("ad", lo, hi), 0.0, A.max, A.add)
+        elif w[0] == "r":
+            ts(ends(rk, rows), ends("cd", rows, 16), v("inv", 1, 2), A.add)
+            send(peer, v("l%s%d" % (half, t)), ends(rk, rows), "a%s%d" % (half, t))
+        elif w[0] == "z":
+            ts(ends("z16", rows), ends(rk, rows), gone, A.add)
+            acp(v("nk", lo, hi), by(v("tab"), ends("z16", rows)))
+        elif w[0] == "q":
+            a0, a1 = int(w[1]), int(w[2])
+            if t == 0 and w == SUMS[0]:
+                qz(v("qg"), v("sg"), v("gs"))
+            qz(v("qc", AT[a0], AT[a1]), v("sc", AT[a0], AT[a1]), v("fl", 4 * AT[a0], 4 * AT[a1]))
+            for a in range(a0, a1):
+                if a < 3:
+                    mm(3, ("qg", "sg"), 0, sums, AT[a] + 128, AT[a + 1], a == 0, a == 2)
+                mm(6, ("qg", "sg"), 0, sums, AT[a], AT[a] + max(128, min(H, WIDE[a])),
+                   w == SUMS[0] and a == a0, w == SUMS[-1] and a == a1 - 1)
+        else:
+            m = int(w[1:])
+            n = 16 * m
+            if w[0] == "c":
+                ts(slot(m, 0, n), bank(4 if m < K else 0, 0, n), score(m), A.is_lt)
+            elif w[0] == "s":
+                scan(v("zv", W * (m + 1) - 8 * m, W * (m + 1)), slot(m, 0, n, 8), slot(m, 0, n, 8, 4), v("ci", m, m + 1), A.add, A.add)
+            elif w[0] == "a":
+                act(v("fs", C * m, C * m + n), bank(5 if m < K else 1, 0, n), AF.Sign, bias=score(m), scale=-1.0)
+            else:
+                act(slot(m, 0, n), v("fs", C * m, C * m + n), AF.Relu, acc=v("acc", m, m + 1))
+
+    SUMS = [w for w in LAYER + COUNT if w[0] == "q" and w[1].isdigit()]
+
+    def children(t):
+        win, rk, la, lb = "win%d" % t, v("rk%d" % t), v("lA%d" % t), v("lB%d" % t)
+
+        def unpack(b):
+            times("S", v(win, 2 * C * b + C, 2 * C * (b + 1)), bank(4 + b), 64.0)
+            if t == 0:
+                times("S", v(win, 2 * C * b, 2 * C * b + C), v("tt0", b, 4 * C, 4), 64.0)
+
+        for b in range(4):
+            mm(4 + b, ("qe", "se"), 128 * b, ("lq%d" % t, "ls%d" % t), 0, C)
+        count("zA", t)
+        ts(v("lo"), rk, gone, A.add, float(M), A.is_lt)
+        ts(v("hi"), rk, gone, A.add, float(C), A.is_ge)
+        ts(v("b1", 2, 4 * Q, 4), rk, -1.0, A.mult, -1.0, A.add)
+        cp(v("b1", 3, 4 * Q, 4), rk)
+        ts(v("st", 2, 3), gone, -float(M), A.add, v("inv", 2, 3), A.mult)
+        tt(v("b0", 3, 4 * Q, 4), v("lo"), v("hi"), A.add)
+        if t == 1:
+            qz(v("qv"), v("sv"), v("vb"))
+        ts(v("v1"), v("b0", 3, 4 * Q, 4), float(C), A.mult)
+        tt(v("v2"), v("v1"), v("x24"), A.add)
+        cp(v("v16"), v("v2"))
+        cp(by(v("np1"), lb), v("nk", H))
+        unpack(0)
+        unpack(1)
+        acp(v("val"), by(v("vtab"), v("v16")))
+        cp(by(v("np1"), la), v("nk", 0, H))
+        scan(v("tc"), v("np1"), v("np1"), 0.0, A.add, A.max)
+        cp(v("tx", 0, H), by(v("tc"), la))
+        acp(v("tx", H), by(v("tc"), lb))
+        unpack(2)
+        unpack(3)
+        scan(v("td"), v("cm"), v("tx"), 0.0, A.mult, A.max)
+        ts(v("b1", 0, 4 * Q, 4), v("td", 15, C, 16), v("inv", 0, 1), A.mult)
+        ts(v("b1", 1, 4 * Q, 4), v("td", 15, C, 16), v("st", 2, 3), A.is_gt, float(L), A.mult)
+        scan(v("bo"), v("b0"), v("b1"), 0.0, A.mult, A.add)
+        cp(v("pl"), v("bo", 3, 4 * Q, 4))
+        cp(by(v("idx"), v("pl")), v("val"))
+        for lo in (0, H):
+            scan(v("idd", lo, lo + H), v("cm", lo, lo + H), v("idx", lo, lo + H), 0.0, A.mult, A.max)
+        for lo in (0, H):
+            ts(v("off", lo // 16, lo // 16 + K), v("idd", lo + 15, lo + H, 16), v("inv", 0, 1), A.mult, -1.0, A.add)
+
+    for t in range(R + 1):
+        for w in LAYER + COUNT:
+            if w in ("qA", "qB"):
+                lo = H if w == "qB" else 0
+                qz(v("qt%d" % t, lo, lo + H), v("sq%d" % t, lo, lo + H), v("tt%d" % t, 4 * lo, 4 * (lo + H)))
+            elif w[0] == "y" or w == "hrow":
+                if t == R:
+                    leave(w)
+            elif w[:2] == "qf" or w in ("wA", "wB") or (w[0] in "gftl" and w[1] in "AB" and len(w) > 2):
+                if t > 0:
+                    layer(w, t)
+            elif t < R:
+                count(w, t)
+        if t < R:
+            children(t)
     schedule(g, T, ops)
     g.sync.wait_ge(T.sem.sto, stores["sto"])
     S.wait_ge(T.sem.sty, stores["sty"])

@@ -5,20 +5,25 @@ STEP = [1, 2, 4]
 Q = C // 16
 H = C // 2
 K = Q // 2
-W = 8 * (Q - 1)
+W = H // 2
 BIG, LOCK, FAR = 1024.0, 4096.0, 1e29
 X4, BF, F32 = "float8_e4m3fn_x4", "bfloat16", "float32"
-QUADS = [[12, 23, 22, 21], [20, 19, 18, 17], [16, 15, 14, 13], [0, 11, 10, 9], [8, 7, 6, 5], [4, 3, 2, 1]]
-WIDE = [C, 320, 256, 192, 128, 64]
+NR = Q + K
+PART = {"A": (0, K), "B": (K, Q), "L": (K, K + K // 2), "U": (K + K // 2, Q)}
+QUADS = [[35, 34, 33, 32], [31, 30, 29, 28], [27, 26, 25, 24], [0, 11, 10, 9], [8, 7, 6, 5], [4, 3, 2, 1], [],
+         [12, 23, 22, 21], [20, 19, 18, 17], [16, 15, 14, 13], []]
+WIDE = [H, H, H, H, 128, 64, 64, H, 128, 64, 64]
 AT = [sum(WIDE[:a]) for a in range(len(WIDE) + 1)]
-NF = AT[-1] + 64
-RUNS = {"A": [[8, 9, 10, 11]], "B": [[13, 15, 17, 19, 21, 23]]}
-LAYER = ("gA2V gA0S gA3V gA1S gB2V gB0S qfA wA gB3V gB1S qfB wB fA0S fA1S fA2S fA3S fB0S fB1S fB2V fB3V tA0 tA1 tA2 tA3 lA0S lA1S lA2S "
-         "tB0 lA3V tB1 lB0S lB1S qA pA yA tB2 tB3 lB2S lB3S mkA ya hrow qB send pF yB yb hdA").split()
-COUNT = ("a11 a10 b11 b10 a9 a8 b9 b8 ownA c7 c6 c5 mkB crA c4 c3 hdB ciA c2 c1 "
-         "a23 a21 b23 b21 a19 a17 b19 b17 a15 a13 b15 b13 n1 n2 n3 "
-         "c22 ownB c12 c20 crB c18 ciB q01 c16 c14 q36 s22 q12 s20 s18 s16 q23 s14 s12 fB s7 s6 xB s5 s4 s3 dB s2 s1 f0 fA rB xA "
-         "zB dA rA").split()
+NF = AT[-1]
+LAYER = ("gA2V gA3V gB2V gA0S gA1S gB0S gB1S qfA wA gB3V qfB wB fA0S fA1S fA2S fA3S fB3V tA0 tA1 tA2 tA3 fB0S fB1S "
+         "lA0S lA1S lA2S fB2S tB0 tB1 lA3V tB3 qA sendA pA lB0S lB1S lB3S tB2 lB2V mkA qB sendB pF hdA").split()
+COUNT = ("c8 a11 a10 a9 b11 b10 b9 ownA mkB c7 c6 hdB a35 a34 h8 a33 b35 a32 b34 a31 a30 a23 b33 b32 b31 b30 "
+         "crA c5 c4 c3 cjA s7 c24 c25 c2 c26 c1 s6 c27 xA s5 c28 ownB s4 s3 c29 s2 s1 q36 c19 uA c18 c17 q23 q01 q12 "
+         "a22 a21 b23 b22 b21 h29 h28 crB c20 c16 s24 c15 c14 s25 c13 cjB dA q7a rA s26 s27 s17 s16 eB s15 vB s14 s13 s18 "
+         "n1 h20 h19 xB uB dB n2 n3 zA nkSA rB lo zB side nkSB w1 jA w2 out w3").split()
+LAST = ("gA2V gA3V gB2V gA0S gA1S gB0S gB1S qfA wA gB3V qfB wB fA0S fA1S fA2S fA3S fB0S fB3V fB2V tA0 tA1 tA2 tA3 fB1S "
+        "lA0S lA1S lA2S lA3S tB0 tB1 tB2 tB3 lB0S lB1S qA yA lB2V lB3V qB hrow yB ya yb").split()
+PLACE = "dA dB jA jB oA oB pA pB sF".split()
 
 SCRATCH = {"ps": ("psum", [128, 4096], F32)}
 for _n, _w, _d in [
@@ -27,19 +32,19 @@ for _n, _w, _d in [
         ("eb", 1056, BF), ("qe", 512, X4), ("se", 512, "uint8"), ("one", 514, BF), ("gb", 512, BF), ("gs", 512, BF),
         ("qg", 128, X4), ("sg", 128, "uint8"),
         ("i16", 16, "int32"), ("r16", 16, "int32"), ("ipm", Q, "int32"), ("rpm", Q, "int32"), ("pm", Q, "uint16"),
-        ("iou", 16, "int32"), ("ou", 16, "uint16"), ("i24", Q, "int32"), ("x24", Q, F32), ("ca", Q, F32),
+        ("iou", 16, "int32"), ("ou", 16, "uint16"), ("i23", Q, "int32"), ("x24", Q, F32), ("ca", Q, F32),
         ("dm16", 16, F32), ("kp16", 16, F32), ("t16", 16, F32), ("c16", 16, F32), ("m16", 16, F32), ("n16", 16, F32),
         ("l16", 16, F32), ("e16", 16, F32), ("a16", 16, F32),
-        ("am", C, F32), ("km", C, F32), ("ad", C, F32), ("kp", C, BF), ("cm", C, BF), ("inv", 4, F32), ("vtab", 2 * C, F32),
+        ("am", C, F32), ("km", C, F32), ("ad", C, F32), ("kp", C, BF), ("cm", C, BF), ("inv", 4, F32),
         ("tab", C + M, BF), ("htab", 2 * C, F32),
-        ("mk", C, F32), ("hold", C, F32), ("cr", C, BF), ("ci", Q, F32), ("acc", Q, F32),
-        ("fl", 4 * NF, BF), ("qc", NF, X4), ("sc", NF, "uint8"), ("zv", Q * W, BF), ("fs", Q * C, BF), ("cd", C, F32),
-        ("cf", C, BF), ("st", 4, F32), ("z16", Q, "uint16"), ("lo", Q, F32), ("hi", Q, F32),
-        ("v1", Q, F32), ("v2", Q, F32), ("v16", Q, "uint16"),
+        ("mk", C, F32), ("row", C, F32), ("hold", C, F32), ("cr", C, BF), ("cj", Q, F32), ("cb", Q, F32), ("acc", NR, F32),
+        ("fl", 4 * NF, BF), ("qc", NF, X4), ("sc", NF, "uint8"), ("zv", NR * W, BF), ("fs", NR * H, BF), ("cd", C, F32),
+        ("cf", C, BF), ("cg", H, BF), ("st", 4, F32), ("z16", Q, "uint16"), ("lo", Q, F32), ("hi", Q, F32),
+        ("v1", Q, F32), ("v2", Q, F32), ("v3", Q, F32), ("x23", Q, F32), ("x25", Q, F32), ("ae", C, F32),
         ("b0", 4 * Q, F32), ("b1", 4 * Q, F32), ("bo", 4 * Q, F32),
-        ("nk", C, BF), ("val", C, F32), ("np1", C, BF), ("tc", C, BF), ("tx", C, BF), ("td", C, BF),
+        ("nk", C, BF), ("val", C, F32), ("npa", C, BF), ("npb", C, BF), ("tc", C, BF), ("tx", C, BF), ("td", C, BF),
         ("pl", Q, "uint16"), ("idx", C, F32), ("idd", C, F32), ("off", Q, "uint16"), ("hrow", C, F32),
-        ("ft", 4 * C, BF), ("f64", 4 * C, BF), ("qf", C, X4), ("sf", C, "uint8"), ("ys", C, F32)]:
+        ("ft", 4 * C, BF), ("f64", 4 * C, BF), ("rs", 4 * C, F32), ("qf", C, X4), ("sf", C, "uint8"), ("ys", C, F32)]:
     SCRATCH[_n] = ("sbuf", [128, _w], _d)
 for _t in range(R + 1):
     SCRATCH["win%d" % _t] = ("sbuf", [128, 8 * C], BF)
@@ -54,7 +59,19 @@ for _t in range(R):
     SCRATCH["lB%d" % _t] = ("sbuf", [128, K], "uint16")
 
 SEMAPHORES = ["V", "S", "P", "G", "lxA", "lxB", "lu", "lv", "lwc", "lws", "sent", "sty", "sto",
-              "ac0", "ac1", "ac2", "aA0", "aA1", "aA2", "aB0", "aB1", "aB2"]
+              "ac0", "ac1", "ac2", "aA0", "aA1", "aA2", "aB0", "aB1", "aB2", "aU0", "aU1", "aU2", "aL0", "aL1", "aL2"]
+
+
+def runs(rows):
+    out = []
+    for m in rows:
+        for run in out:
+            if len(run) == 1 or m - run[-1] == run[1] - run[0]:
+                run.append(m)
+                break
+        else:
+            out.append([m])
+    return out
 
 
 def clash(a, b):
@@ -72,13 +89,20 @@ def schedule(g, T, ops):
     queues = {"V": g.vector, "S": g.scalar, "P": g.tensor, "G": g, "Y": g.sync}
     known = {q: {} for q in queues}
     pos = {q: 0 for q in queues}
+    issued = {}
     for n, o in enumerate(ops):
         q = o["q"]
         o["waits"] = []
         if q is not None:
-            for d in range(n - 1, -1, -1):
+            need = []
+            for tok, done in issued.items():
+                for d in done[known[q].get(tok, 0):][::-1]:
+                    if clash(ops[d], o):
+                        need.append(d)
+                        break
+            for d in sorted(need, reverse=True):
                 e = ops[d]
-                if e["tok"] is None or known[q].get(e["tok"], 0) >= e["at"] or not clash(e, o):
+                if known[q].get(e["tok"], 0) >= e["at"]:
                     continue
                 o["waits"].append(d)
                 e["inc"] = True
@@ -95,6 +119,7 @@ def schedule(g, T, ops):
         o["clock"] = dict(known[q]) if q is not None else {}
         if o["tok"] is not None:
             o["clock"][o["tok"]] = o["at"]
+            issued.setdefault(o["tok"], []).append(n)
     count = {q: 0 for q in queues}
     for o in ops:
         if o["q"] is None:
@@ -214,62 +239,62 @@ def rank_program(g, core, T, topo):
     load("S", v("ub"), T.u[:], "lu")
     load("Y", v("tt0", 0, 4 * H), T.x[:, 0:4 * H], "lxA")
     load("Y", v("tt0", 4 * H), T.x[:, 4 * H:4 * C], "lxB")
-    load("Y", raw(v("qw"), dt.uint8), T.wc[:], "lwc", [v("tt0")])
-    load("Y", v("sw"), T.ws[:], "lws")
-    load("Y", v("vb"), T.v[:], "lv")
 
     iota(v("i16"), [[1, 16]], 128, -1)
     iota(v("ipm"), [[0, Q]], 0, 1)
     iota(v("iou"), [[1, 2], [16, 8]], 0, 0)
-    iota(v("i24"), [[16, Q]], 0, 0)
+    iota(v("i23"), [[-16, Q]], H - 15, 0)
     ms(v("one"), 1.0)
-    for b in range(2):
-        keep(v("eb", 528 * b, 528 * b + 514), v("one"), [[1, 514]], -2 - b, -4, A.is_equal)
     keep(v("gb"), v("one", 0, 512), [[16, 8], [0, 64]], 15, -1, A.is_ge)
     keep(v("gs"), v("gb"), [[-16, 8], [0, 64]], 0, 1, A.is_ge)
-    ms(v("fl", 4 * AT[-2]), 0.0)
+    keep(v("eb", 0, 514), v("one"), [[1, 514]], -2, -4, A.is_equal)
+    ms(v("fl", 4 * AT[5], 4 * AT[7]), 0.0)
     ts(v("r16"), v("i16"), 15, A.bitwise_and)
     ts(v("rpm"), v("ipm"), 15, A.bitwise_and)
     ms(v("n16", 0, 1), -FAR)
-    ms(v("b0"), 1.0)
+    for lo, hi, x in ((0, M, 1.0), (M, C, 0.0), (C, C + M, 1.0)):
+        times("S", v("tab", lo, hi), v("one", 0, hi - lo), x)
     ts(v("dm16"), v("r16"), 0, A.is_equal)
     cp(v("pm"), v("rpm"))
-    ts(v("kp16"), v("r16"), 0, A.not_equal)
-    ts(v("t16"), v("r16"), 1.0, A.is_equal, BIG, A.mult)
-    ts(v("l16"), v("r16"), 15.0, A.is_equal, -LOCK, A.mult)
+    cp(v("ou"), v("iou"))
     ts(v("m16"), v("dm16"), 2 * FAR, A.mult, -FAR, A.add)
     ts(v("n16", 1), v("dm16", 1), -2 * FAR, A.mult, FAR, A.add)
+    ts(v("kp16"), v("r16"), 0, A.not_equal)
+    ts(v("l16"), v("r16"), 15.0, A.is_equal, -LOCK, A.mult)
     ts(v("e16"), v("dm16"), BIG, A.mult)
-    cp(v("ou"), v("iou"))
-    tt(v("c16"), v("t16"), v("kp16"), A.max)
     acp(v("am"), by(v("m16"), v("pm")))
     acp(v("km"), by(v("n16"), v("pm")))
-    acp(v("kp"), by(v("kp16"), v("pm")))
+    tt(v("ca"), v("rpm"), v("i23"), A.add)
+    ms(v("acc"), 0.0)
     tt(v("a16"), v("e16"), v("l16"), A.add)
-    last = v("dm16", 15, 16)
-    ts(v("inv", 0, 1), last, 1.0 - 1.0 / BIG, A.mult, 1.0 / BIG, A.add)
     ts(v("inv", 1, 2), v("dm16", 0, 1), LOCK, A.mult, H - BIG, A.add)
-    ts(v("inv", 2, 3), last, BIG - 1.0, A.mult, -BIG, A.add)
-    tt(v("x24"), v("i24"), v("rpm"), A.add)
-    tt(v("ca"), v("rpm"), v("i24"), A.subtract)
-    ms(v("b0", 0, 4 * Q, 4), 0.0)
-    for a in range(len(QUADS) - 1):
+    ms(v("fl", 4 * AT[9]), 0.0)
+    qz(v("qc", AT[5], AT[7]), v("sc", AT[5], AT[7]), v("fl", 4 * AT[5], 4 * AT[7]))
+    for a in (3, 4, 7, 8):
         ms(v("fl", 4 * (AT[a + 1] - 48), 4 * AT[a + 1]), 0.0)
-    ts(v("ca"), v("ca"), float(H - 15), A.add)
     qz(v("qu"), v("su"), v("ub"))
-    qz(v("qc", AT[-2]), v("sc", AT[-2]), v("fl", 4 * AT[-2]))
-    cp(raw(v("qp"), dt.uint32), by(v("qu"), v("ou"), True))
-    acp(v("sp"), by(v("su"), v("ou")))
+    qz(v("qc", AT[9]), v("sc", AT[9]), v("fl", 4 * AT[9]))
+    ts(v("cb"), v("ca"), -1.0, A.mult, v("a16", 15, 16), A.add)
+    ts(v("t16"), v("r16"), 1.0, A.is_equal, BIG, A.mult)
+    tt(v("x23"), v("rpm"), v("i23"), A.subtract)
+    ts(v("inv", 3, 4), v("dm16", 0, 1), LOCK, A.mult, -BIG, A.add)
+    for c in (0, 8):
+        cp(raw(v("qp", 16 * c, 16 * c + 128), dt.uint32), by(v("qu"), v("ou", c, c + 8), True))
+        acp(v("sp", 16 * c, 16 * c + 128), by(v("su"), v("ou", c, c + 8)))
+    tt(v("c16"), v("t16"), v("kp16"), A.max)
+    ts(v("x24"), v("x23"), float(H - 15), A.add)
+    ts(v("x25"), v("x23"), float(H - 15 - L), A.add)
+    acp(v("kp"), by(v("kp16"), v("pm")))
     acp(v("ad"), by(v("a16"), v("pm")))
-    acp(v("cm"), by(v("c16"), v("pm")))
-    for b in range(4):
-        lo = 528 * (b % 2) + 2 - b // 2 * 2
-        qz(v("qe", 128 * b, 128 * (b + 1)), v("se", 128 * b, 128 * (b + 1)), v("eb", lo, lo + 512))
 
-    def slot(m, lo, hi, step=4, first=0):
+    def unit(b):
+        at = 528 * (b % 2) + 2 - b // 2 * 2
+        qz(v("qe", 128 * b, 128 * (b + 1)), v("se", 128 * b, 128 * (b + 1)), v("eb", at, at + 512))
+
+    def slot(m, n, step=4, first=0):
         a = [m in rows for rows in QUADS].index(True)
         at = 4 * AT[a] + QUADS[a].index(m)
-        return v("fl", at + 4 * lo + first, at + 4 * hi, step)
+        return v("fl", at + first, at + 4 * n, step)
 
     def ends(name, rows, w=1):
         step = rows[1] - rows[0] if len(rows) > 1 else 1
@@ -279,6 +304,9 @@ def rank_program(g, core, T, topo):
         return v("hold", 16 * m + 15, 16 * m + 16)
 
     up, sums, gone = ("qp", "sp"), ("qc", "sc"), v("st", 1, 2)
+
+    def scale(b):
+        return 64.0 if "tA%d" % b in LAYER else 1.0
 
     def layer(w, t):
         lo = H if "B" in w else 0
@@ -293,8 +321,13 @@ def rank_program(g, core, T, topo):
         b = int(w[2])
         part, big = v("ft", 4 * lo + b, 4 * hi, 4), v("f64", C * b + lo, C * b + hi)
         new = v("win%d" % t, 2 * C * b + lo, 2 * C * b + hi)
+        picked = by(v("win%d" % (t - 1), 2 * C * b, 2 * C * (b + 1)), v("off", lo // 16, hi // 16))
         if w[0] == "g":
-            times(w[3], part, by(v("win%d" % (t - 1), 2 * C * b, 2 * C * (b + 1)), v("off", lo // 16, hi // 16)), 0.015625)
+            times(w[3], part, picked, 1.0 / scale(b))
+        elif w[0] == "i":
+            times("S", v("rs", C * b + lo, C * b + hi), bank(b if lo else 4 + b, 0, H), 0.015625)
+        elif w[0] == "k":
+            tt(v("tt%d" % t, 4 * lo + b, 4 * hi, 4), picked, v("rs", C * b + lo, C * b + hi), A.add)
         elif w[0] == "f":
             times(w[3], big, part, 64.0)
         elif w[0] == "t":
@@ -324,136 +357,184 @@ def rank_program(g, core, T, topo):
         peer = T.cores[rank ^ STEP[t]]
         state, rk = ("qt%d" % t, "sq%d" % t), "rk%d" % t
         half = w[-1]
-        lo = H if half == "B" else 0
-        hi, rows = lo + H, list(range(lo // 16, lo // 16 + K))
-        scores = bank(0, H) if lo else bank(4, 0, H)
-        if w == "send":
+        rows = list(range(*PART.get(half, PART["A"])))
+        lo, hi = 16 * rows[0], 16 * rows[-1] + 16
+        land = v("lA%d" % t) if half == "A" else v("lB%d" % t, rows[0] % K, rows[-1] % K + 1)
+        scores = bank(0 if lo else 4, 0, H)
+        if w[:4] == "send":
+            send(peer, raw(v("lq%d" % t, lo, hi), dt.uint8), raw(v(state[0], lo, hi), dt.uint8), "ac%d" % t)
+            if not lo:
+                return
             ne = len(topo.engines(peer, core))
             lq, ls = v("lq%d" % t), v("ls%d" % t)
-            send(peer, raw(lq, dt.uint8), raw(v(state[0]), dt.uint8), "ac%d" % t)
             send(peer, ls, v(state[1]), "ac%d" % t)
-            op(None, None, [lq, ls], [], sem="ac%d" % t, val=2 * ne)
-            for h in "AB":
-                op(None, None, [v("l%s%d" % (h, t))], [], sem="a%s%d" % (h, t), val=ne)
+            op(None, None, [lq, ls], [], sem="ac%d" % t, val=3 * ne)
+            for h in "ABUL":
+                if "r" + h in LAYER + COUNT:
+                    op(None, None, [v("l%s%d" % ("AB"[h != "A"], t), PART[h][0] % K, (PART[h][1] - 1) % K + 1)], [],
+                       sem="a%s%d" % (h, t), val=ne)
             if t == 0:
-                for a, b, x in ((0, M, 1), (M, C, 0), (C, C + M, 1)):
-                    iota(v("tab", a, b), [[0, b - a]], x, 0, real=True)
-                iota(v("vtab"), [[1, 2 * C]], 1, 0, real=True)
+                keep(v("eb", 528, 528 + 514), v("one"), [[1, 514]], -3, -4, A.is_equal)
+                iota(v("val"), [[1, C]], 0, 0, real=True)
             if t == 1:
                 iota(v("htab"), [[0, 2], [1, C]], 0, 0, real=True)
         elif w == "pA":
             mm(4, up, 0, state, 0, H)
             mm(5, up, 0, state, 0, H)
+            if t == 0:
+                qz(v("qg"), v("sg"), v("gs"))
         elif w == "pF":
-            for b, c in ((0, 0), (2, 128), (1, 0)):
-                mm(b, up, c, state, 0, C)
+            mm(0, up, 0, state, H, C)
+            mm(1, up, 0, state, H, C)
+            mm(2, up, 128, state, 0, C)
+        elif w[:3] == "row":
+            acp(v("row", lo, hi), bank(1 if lo else 5, 0, H))
         elif w[:2] == "mk":
             tt(v("mk", lo, hi), scores, v("am", lo, hi), A.min)
         elif w[:2] == "hd":
             scan(v("hold", lo, hi), v("km", lo, hi), v("mk", lo, hi), 0.0, A.min, A.max)
         elif w[:3] == "own":
-            tt(slot(lo // 16, lo, hi), scores, v("hold", lo, hi), A.is_le)
+            tt(slot(lo // 16, H), scores, v("hold", lo, hi), A.is_le)
         elif w[:2] == "cr":
-            scan(v("cr", lo, hi), v("kp", lo, hi), slot(lo // 16, lo, hi), 0.0, A.mult, A.add)
-        elif w[:2] == "ci":
-            tt(ends("ci", rows), ends("cr", rows, 16), ends("ca", rows), A.add)
+            scan(v("cr", lo, hi), v("kp", lo, hi), slot(lo // 16, H), 0.0, A.mult, A.add)
         elif w == "n1":
             act(v("cf"), bank(2), AF.Sign)
         elif w == "n2":
             act(v("cf"), v("cf"), AF.Relu, acc=v("st", 0, 1))
         elif w == "n3":
-            act(gone, v("st", 0, 1), AF.Relu, bias=float(M), scale=-1.0)
-        elif w == "f0":
-            cp(ends("zv", [0], W), v("ci", 0, 1))
-        elif w[0] == "f":
-            for run in RUNS[half]:
-                tt(ends("zv", run, W), ends("acc", run), ends("ci", run), A.add)
-        elif w[0] == "x":
-            ts(ends("ad", rows, 16), ends("zv", rows, W), -1.0, A.mult, v("a16", 15, 16), A.add)
+            ts(gone, v("st", 0, 1), float(M), A.min)
+        elif w == "lo":
+            if t == 0:
+                ms(v("b0"), 1.0)
+                acp(v("ae"), by(v("a16"), v("pm")))
+                ts(v("inv", 0, 1), v("dm16", 15, 16), 1.0 - 1.0 / BIG, A.mult, 1.0 / BIG, A.add)
+                ts(v("inv", 2, 3), v("dm16", 15, 16), 1.0 - BIG, A.mult, BIG, A.add)
+                ms(v("b0", 0, 4 * Q, 4), 0.0)
+            ts(v("lo"), v(rk), gone, A.is_lt)
+            ts(v("hi"), v(rk), gone, A.subtract, float(L), A.is_ge)
+            ts(v("b1", 2, 4 * Q, 4), v(rk), -1.0, A.mult, -1.0, A.add)
+            cp(v("b1", 3, 4 * Q, 4), v(rk))
+            ts(v("st", 2, 3), gone, v("inv", 2, 3), A.mult)
+        elif w == "out":
+            tt(v("b0", 3, 4 * Q, 4), v("lo"), v("hi"), A.add)
+        elif w == "w1":
+            ts(v("v1"), v("x24"), gone, A.is_lt, float(C), A.mult)
+            ts(v("v2"), v("x25"), gone, A.is_ge, float(C), A.mult)
+        elif w == "w2":
+            tt(v("v3"), v("v1"), v("v2"), A.add)
+        elif w == "w3":
+            ts(v("ae", 15, C, 16), v("v3"), v("a16", 15, 16), A.add)
+        elif w[0] == "j":
+            cp(by(v("npa"), land), v("nk", lo, hi))
+        elif w == "side":
+            for b in range(4 if t == 0 else 0):
+                unit(b)
+            if t == 1:
+                qz(v("qv"), v("sv"), v("vb"))
+        elif w[:2] == "cj":
+            tt(ends("cj", rows), ends("cb", rows), ends("cr", rows, 16), A.subtract)
+        elif w[0] in "xu":
+            for run in runs([m for m in rows if ("s%d" % m in COUNT + LAYER) == (w[0] == "u")]):
+                tt(ends("ad", run, 16), ends("cj", run), ends("acc", run) if w[0] == "x" else ends("zv", run, W), A.subtract)
+        elif w[0] in "ev":
+            for run in runs([m for m in rows if ("s%d" % (m + K) in COUNT + LAYER) == (w[0] == "v")]):
+                far = [m + K for m in run]
+                tt(ends("cj", run), ends("cj", run), ends("acc", far) if w[0] == "e" else ends("zv", far, W), A.subtract)
         elif w[0] == "d":
-            scan(v("cd", lo, hi), bank(3, H - 128, C - 128) if lo else bank(6, 0, H), v("ad", lo, hi), 0.0, A.max, A.add)
+            scan(v("cd", lo, hi), bank({"A": 6, "L": 7}.get(half, 3), lo % H, lo % H + hi - lo), v("ad", lo, hi), 0.0, A.max, A.add)
         elif w[0] == "r":
             ts(ends(rk, rows), ends("cd", rows, 16), v("inv", 1, 2), A.add)
-            send(peer, v("l%s%d" % (half, t)), ends(rk, rows), "a%s%d" % (half, t))
+            send(peer, land, ends(rk, rows), "a%s%d" % (half, t))
         elif w[0] == "z":
-            ts(ends("z16", rows), ends(rk, rows), gone, A.add)
-            acp(v("nk", lo, hi), by(v("tab"), ends("z16", rows)))
+            ts(ends("z16", rows), ends(rk, rows), gone, A.subtract, float(M), A.add)
+        elif w[:2] == "nk":
+            (cp if w[2] == "V" else acp)(v("nk", lo, hi), by(v("tab"), ends("z16", rows)))
         elif w[0] == "q":
-            a0, a1 = int(w[1]), int(w[2])
-            if t == 0 and w == SUMS[0]:
-                qz(v("qg"), v("sg"), v("gs"))
+            a0, a1 = int(w[1], 16), int(w[2], 16)
             qz(v("qc", AT[a0], AT[a1]), v("sc", AT[a0], AT[a1]), v("fl", 4 * AT[a0], 4 * AT[a1]))
+            same = [x for x in LAYER + COUNT if x[0] == "q" and x[1].isdigit() and (x[1] > "6") == (a0 > 6)]
+            if a0 > 6 and "rU" in LAYER + COUNT:
+                for a in range(a0, min(a1, 9)):
+                    mm(3, ("qg", "sg"), 0, sums, AT[a], AT[a + 1], a == 7, a == 8)
+                for a in range(a0, min(a1, 10)):
+                    mm(7, ("qg", "sg"), 0, sums, AT[a], AT[a] + 128, a == 7, a == 9)
+                return
             for a in range(a0, a1):
-                if a < 3:
-                    mm(3, ("qg", "sg"), 0, sums, AT[a] + 128, AT[a + 1], a == 0, a == 2)
-                mm(6, ("qg", "sg"), 0, sums, AT[a], AT[a] + max(128, min(H, WIDE[a])),
-                   w == SUMS[0] and a == a0, w == SUMS[-1] and a == a1 - 1)
+                mm(3 if a0 > 6 else 6, ("qg", "sg"), 0, sums, AT[a], AT[a] + max(128, WIDE[a]),
+                   w == same[0] and a == a0, w == same[-1] and a == a1 - 1)
         else:
             m = int(w[1:])
-            n = 16 * m
+            n, upper = (16 * (m % K), m >= K) if m < Q else (H, False)
+            mine = score(m if m < Q else m - K)
+            row = v("row", H * upper, H * upper + n) if "row" + "AB"[upper] in LAYER + COUNT else None
             if w[0] == "c":
-                ts(slot(m, 0, n), bank(4 if m < K else 0, 0, n), score(m), A.is_lt)
+                ts(slot(m, n), row or bank(0 if upper else 4, 0, n), mine, A.is_lt)
             elif w[0] == "s":
-                scan(v("zv", W * (m + 1) - 8 * m, W * (m + 1)), slot(m, 0, n, 8), slot(m, 0, n, 8, 4), v("ci", m, m + 1), A.add, A.add)
+                scan(v("zv", W * (m + 1) - n // 2, W * (m + 1)), slot(m, n, 8), slot(m, n, 8, 4), 0.0, A.add, A.add)
+            elif w[0] == "h":
+                act(v("fs", H * m, H * m + n), slot(m, n), AF.Relu, acc=v("acc", m, m + 1))
             elif w[0] == "a":
-                act(v("fs", C * m, C * m + n), bank(5 if m < K else 1, 0, n), AF.Sign, bias=score(m), scale=-1.0)
+                act(v("fs", H * m, H * m + n), row or bank(1 if upper else 5, 0, n), AF.Sign, bias=mine, scale=-1.0)
             else:
-                act(slot(m, 0, n), v("fs", C * m, C * m + n), AF.Relu, acc=v("acc", m, m + 1))
-
-    SUMS = [w for w in LAYER + COUNT if w[0] == "q" and w[1].isdigit()]
+                act(slot(m, n), v("fs", H * m, H * m + n), AF.Relu, acc=v("acc", m, m + 1))
 
     def children(t):
         win, rk, la, lb = "win%d" % t, v("rk%d" % t), v("lA%d" % t), v("lB%d" % t)
 
-        def unpack(b):
-            times("S", v(win, 2 * C * b + C, 2 * C * (b + 1)), bank(4 + b), 64.0)
-            if t == 0:
-                times("S", v(win, 2 * C * b, 2 * C * b + C), v("tt0", b, 4 * C, 4), 64.0)
+        def planes(b0, b1):
+            for b in range(b0, b1):
+                if t == 0 or scale(b) == 1.0:
+                    times("S", v(win, 2 * C * b, 2 * C * b + C), v("tt%d" % t, b, 4 * C, 4), scale(b))
 
+        if t == 0:
+            acp(v("cm"), by(v("c16"), v("pm")))
+            load("Y", raw(v("qw"), dt.uint8), T.wc[:], "lwc", [v("b0")])
+            load("Y", v("sw"), T.ws[:], "lws")
         for b in range(4):
             mm(4 + b, ("qe", "se"), 128 * b, ("lq%d" % t, "ls%d" % t), 0, C)
-        count("zA", t)
-        ts(v("lo"), rk, gone, A.add, float(M), A.is_lt)
-        ts(v("hi"), rk, gone, A.add, float(C), A.is_ge)
-        ts(v("b1", 2, 4 * Q, 4), rk, -1.0, A.mult, -1.0, A.add)
-        cp(v("b1", 3, 4 * Q, 4), rk)
-        ts(v("st", 2, 3), gone, -float(M), A.add, v("inv", 2, 3), A.mult)
-        tt(v("b0", 3, 4 * Q, 4), v("lo"), v("hi"), A.add)
-        if t == 1:
-            qz(v("qv"), v("sv"), v("vb"))
-        ts(v("v1"), v("b0", 3, 4 * Q, 4), float(C), A.mult)
-        tt(v("v2"), v("v1"), v("x24"), A.add)
-        cp(v("v16"), v("v2"))
-        cp(by(v("np1"), lb), v("nk", H))
-        unpack(0)
-        unpack(1)
-        acp(v("val"), by(v("vtab"), v("v16")))
-        cp(by(v("np1"), la), v("nk", 0, H))
-        scan(v("tc"), v("np1"), v("np1"), 0.0, A.add, A.max)
+        planes(0, 2)
+        count("jL" if "rU" in LAYER + COUNT else "jB", t)
+        scan(v("tc"), v("npa"), v("npa"), 0.0, A.add, A.max)
         cp(v("tx", 0, H), by(v("tc"), la))
         acp(v("tx", H), by(v("tc"), lb))
-        unpack(2)
-        unpack(3)
-        scan(v("td"), v("cm"), v("tx"), 0.0, A.mult, A.max)
-        ts(v("b1", 0, 4 * Q, 4), v("td", 15, C, 16), v("inv", 0, 1), A.mult)
-        ts(v("b1", 1, 4 * Q, 4), v("td", 15, C, 16), v("st", 2, 3), A.is_gt, float(L), A.mult)
-        scan(v("bo"), v("b0"), v("b1"), 0.0, A.mult, A.add)
-        cp(v("pl"), v("bo", 3, 4 * Q, 4))
-        cp(by(v("idx"), v("pl")), v("val"))
+        planes(2, 4)
+        for b in range(4):
+            times("S", v(win, 2 * C * b + C, 2 * C * (b + 1)), bank(4 + b), scale(b))
+
+        def step(w):
+            lo = H if w[1] == "B" else 0
+            b = lo // 4
+            if w[0] == "d":
+                scan(v("td", lo, lo + H), v("cm", lo, lo + H), v("tx", lo, lo + H), 0.0, A.mult, A.max)
+            elif w[0] == "j":
+                ts(v("b1", b, b + 4 * K, 4), v("td", lo + 15, lo + H, 16), v("inv", 0, 1), A.mult)
+                ts(v("b1", b + 1, b + 4 * K, 4), v("td", lo + 15, lo + H, 16), v("st", 2, 3), A.is_gt, float(L), A.mult)
+            elif w[0] == "o":
+                scan(v("bo", b, b + 4 * K), v("b0", b, b + 4 * K), v("b1", b, b + 4 * K), 0.0, A.mult, A.add)
+            elif w[0] == "p":
+                cp(v("pl", lo // 16, lo // 16 + K), v("bo", b + 3, b + 4 * K, 4))
+            else:
+                cp(by(v("idx"), v("pl")), v("val"))
+
+        for w in PLACE:
+            step(w)
         for lo in (0, H):
-            scan(v("idd", lo, lo + H), v("cm", lo, lo + H), v("idx", lo, lo + H), 0.0, A.mult, A.max)
+            scan(v("idd", lo, lo + H), v("idx", lo, lo + H), v("ae", lo, lo + H), 0.0, A.max, A.add)
         for lo in (0, H):
-            ts(v("off", lo // 16, lo // 16 + K), v("idd", lo + 15, lo + H, 16), v("inv", 0, 1), A.mult, -1.0, A.add)
+            ts(v("off", lo // 16, lo // 16 + K), v("idd", lo + 15, lo + H, 16), v("inv", 3, 4), A.add)
+        if t == 0:
+            load("Y", v("vb"), T.v[:], "lv", [v("off")])
 
     for t in range(R + 1):
-        for w in LAYER + COUNT:
+        order = LAYER + COUNT if t < R else LAST
+        for w in order:
             if w in ("qA", "qB"):
                 lo = H if w == "qB" else 0
                 qz(v("qt%d" % t, lo, lo + H), v("sq%d" % t, lo, lo + H), v("tt%d" % t, 4 * lo, 4 * (lo + H)))
             elif w[0] == "y" or w == "hrow":
                 if t == R:
                     leave(w)
-            elif w[:2] == "qf" or w in ("wA", "wB") or (w[0] in "gftl" and w[1] in "AB" and len(w) > 2):
+            elif w[:2] == "qf" or w in ("wA", "wB") or (w[0] in "gftlik" and w[1] in "AB" and len(w) > 2):
                 if t > 0:
                     layer(w, t)
             elif t < R:

from concourse.mybir import dt, AluOpType as A, ActivationFunctionType as AF

C, L, M, R = 384, 160, 224, 3
STEP = [1, 2, 4]
Q = C // 16
H = C // 2
K = Q // 2
W = H // 2
BIG, LOCK, FAR = 1024.0, 4096.0, 1e29
X4, BF, F32 = "float8_e4m3fn_x4", "bfloat16", "float32"
NR = Q + K
PART = {"A": (0, K), "B": (K, Q), "L": (K, K + K // 2), "U": (K + K // 2, Q)}
QUADS = [[35, 34, 33, 32], [31, 30, 29, 28], [27, 26, 25, 24], [0, 11, 10, 9], [8, 7, 6, 5], [4, 3, 2, 1], [],
         [12, 23, 22, 21], [20, 19, 18, 17], [16, 15, 14, 13], []]
WIDE = [H, H, H, H, 128, 64, 64, H, 128, 64, 64]
AT = [sum(WIDE[:a]) for a in range(len(WIDE) + 1)]
NF = AT[-1]
LAYER = ("gA2V gA3V gB2V gA0S gA1S gB0S gB1S qfA wA gB3V qfB wB fA0S fA1S fA2S fA3S fB3V tA0 tA1 tA2 tA3 fB0S fB1S "
         "lA0S lA1S lA2S fB2S tB0 tB1 lA3V tB3 qA sendA pA lB0S lB1S lB3S tB2 lB2V mkA qB sendB pF hdA").split()
COUNT = ("c8 a11 a10 a9 b11 b10 b9 ownA mkB c7 c6 hdB a35 a34 h8 a33 b35 a32 b34 a31 a30 a23 b33 b32 b31 b30 "
         "crA c5 c4 c3 cjA s7 c24 c25 c2 c26 c1 s6 c27 xA s5 c28 ownB s4 s3 c29 s2 s1 q36 c19 uA c18 c17 q23 q01 q12 "
         "a22 a21 b23 b22 b21 h29 h28 crB c20 c16 s24 c15 c14 s25 c13 cjB dA q7a rA s26 s27 s17 s16 eB s15 vB s14 s13 s18 "
         "n1 h20 h19 xB uB dB n2 n3 zA nkSA rB lo zB side nkSB w1 jA w2 out w3").split()
LAST = ("gA2V gA3V gB2V gA0S gA1S gB0S gB1S qfA wA gB3V qfB wB fA0S fA1S fA2S fA3S fB0S fB3V fB2V tA0 tA1 tA2 tA3 fB1S "
        "lA0S lA1S lA2S lA3S tB0 tB1 tB2 tB3 lB0S lB1S qA yA lB2V lB3V qB hrow yB ya yb").split()
PLACE = "dA dB jA jB oA oB pA pB sF".split()

SCRATCH = {"ps": ("psum", [128, 4096], F32)}
for _n, _w, _d in [
        ("ub", 512, BF), ("vb", 512, BF), ("qu", 128, X4), ("su", 128, "uint8"), ("qp", 256, X4), ("sp", 256, "uint8"),
        ("qv", 128, X4), ("sv", 128, "uint8"), ("qw", 512, X4), ("sw", 512, "uint8"),
        ("eb", 1056, BF), ("qe", 512, X4), ("se", 512, "uint8"), ("one", 514, BF), ("gb", 512, BF), ("gs", 512, BF),
        ("qg", 128, X4), ("sg", 128, "uint8"),
        ("i16", 16, "int32"), ("r16", 16, "int32"), ("ipm", Q, "int32"), ("rpm", Q, "int32"), ("pm", Q, "uint16"),
        ("iou", 16, "int32"), ("ou", 16, "uint16"), ("i23", Q, "int32"), ("x24", Q, F32), ("ca", Q, F32),
        ("dm16", 16, F32), ("kp16", 16, F32), ("t16", 16, F32), ("c16", 16, F32), ("m16", 16, F32), ("n16", 16, F32),
        ("l16", 16, F32), ("e16", 16, F32), ("a16", 16, F32),
        ("am", C, F32), ("km", C, F32), ("ad", C, F32), ("kp", C, BF), ("cm", C, BF), ("inv", 4, F32),
        ("tab", C + M, BF), ("htab", 2 * C, F32),
        ("mk", C, F32), ("row", C, F32), ("hold", C, F32), ("cr", C, BF), ("cj", Q, F32), ("cb", Q, F32), ("acc", NR, F32),
        ("fl", 4 * NF, BF), ("qc", NF, X4), ("sc", NF, "uint8"), ("zv", NR * W, BF), ("fs", NR * H, BF), ("cd", C, F32),
        ("cf", C, BF), ("cg", H, BF), ("st", 4, F32), ("z16", Q, "uint16"), ("lo", Q, F32), ("hi", Q, F32),
        ("v1", Q, F32), ("v2", Q, F32), ("v3", Q, F32), ("x23", Q, F32), ("x25", Q, F32), ("ae", C, F32),
        ("b0", 4 * Q, F32), ("b1", 4 * Q, F32), ("bo", 4 * Q, F32),
        ("nk", C, BF), ("val", C, F32), ("npa", C, BF), ("npb", C, BF), ("tc", C, BF), ("tx", C, BF), ("td", C, BF),
        ("pl", Q, "uint16"), ("idx", C, F32), ("idd", C, F32), ("off", Q, "uint16"), ("hrow", C, F32),
        ("ft", 4 * C, BF), ("f64", 4 * C, BF), ("rs", 4 * C, F32), ("qf", C, X4), ("sf", C, "uint8"), ("ys", C, F32)]:
    SCRATCH[_n] = ("sbuf", [128, _w], _d)
for _t in range(R + 1):
    SCRATCH["win%d" % _t] = ("sbuf", [128, 8 * C], BF)
    SCRATCH["tt%d" % _t] = ("sbuf", [128, 4 * C], BF)
    SCRATCH["qt%d" % _t] = ("sbuf", [128, C], X4)
    SCRATCH["sq%d" % _t] = ("sbuf", [128, C], "uint8")
for _t in range(R):
    SCRATCH["lq%d" % _t] = ("sbuf", [128, C], X4)
    SCRATCH["ls%d" % _t] = ("sbuf", [128, C], "uint8")
    SCRATCH["rk%d" % _t] = ("sbuf", [128, Q], "uint16")
    SCRATCH["lA%d" % _t] = ("sbuf", [128, K], "uint16")
    SCRATCH["lB%d" % _t] = ("sbuf", [128, K], "uint16")

SEMAPHORES = ["V", "S", "P", "G", "lxA", "lxB", "lu", "lv", "lwc", "lws", "sent", "sty", "sto",
              "ac0", "ac1", "ac2", "aA0", "aA1", "aA2", "aB0", "aB1", "aB2", "aU0", "aU1", "aU2", "aL0", "aL1", "aL2"]


def runs(rows):
    out = []
    for m in rows:
        for run in out:
            if len(run) == 1 or m - run[-1] == run[1] - run[0]:
                run.append(m)
                break
        else:
            out.append([m])
    return out


def clash(a, b):
    if a["names"] & b["names"]:
        for n, m in a["w"]:
            if any(n == k and m & x for k, x in b["r"] + b["w"]):
                return not (a["sum"] and b["sum"])
        for n, m in a["r"]:
            if any(n == k and m & x for k, x in b["w"]):
                return True
    return a["q"] != b["q"] and bool(a["banks"] & b["banks"])


def schedule(g, T, ops):
    queues = {"V": g.vector, "S": g.scalar, "P": g.tensor, "G": g, "Y": g.sync}
    known = {q: {} for q in queues}
    pos = {q: 0 for q in queues}
    issued = {}
    for n, o in enumerate(ops):
        q = o["q"]
        o["waits"] = []
        if q is not None:
            need = []
            for tok, done in issued.items():
                for d in done[known[q].get(tok, 0):][::-1]:
                    if clash(ops[d], o):
                        need.append(d)
                        break
            for d in sorted(need, reverse=True):
                e = ops[d]
                if known[q].get(e["tok"], 0) >= e["at"]:
                    continue
                o["waits"].append(d)
                e["inc"] = True
                for k, v in e["clock"].items():
                    if known[q].get(k, 0) < v:
                        known[q][k] = v
        if o["sem"] is not None:
            o["tok"], o["at"] = o["sem"], 1
        elif o["loose"]:
            o["tok"], o["at"] = None, 0
        else:
            pos[q] += 1
            o["tok"], o["at"] = q, pos[q]
        o["clock"] = dict(known[q]) if q is not None else {}
        if o["tok"] is not None:
            o["clock"][o["tok"]] = o["at"]
            issued.setdefault(o["tok"], []).append(n)
    count = {q: 0 for q in queues}
    for o in ops:
        if o["q"] is None:
            continue
        for d in o["waits"]:
            e = ops[d]
            queues[o["q"]].wait_ge(T.sem[e["tok"]], e["val"])
        ins = o["f"]()
        if o["sem"] is not None:
            ins.then_inc(T.sem[o["sem"]], 16)
        elif o.get("inc"):
            count[o["q"]] += 1
            o["val"] = count[o["q"]]
            ins.then_inc(T.sem[o["q"]], 1)


def rank_program(g, core, T, topo):
    rank = T.rank_of(core)
    if rank is None:
        return
    ops = []
    V, S = g.vector, g.scalar

    def v(name, lo=0, hi=None, step=1):
        hi = SCRATCH[name][1][1] if hi is None else hi
        mask = sum(1 << c for c in range(lo, hi, step)) if step > 1 else (1 << hi) - (1 << lo)
        return (T[name][:, lo:hi:step] if step > 1 else T[name][:, lo:hi], [(name, mask)], [])

    def by(win, off, words=False):
        ap = win[0].bitcast(dt.uint32) if words else win[0]
        return (ap.indirect(off[0]), win[1], off[1])

    def raw(x, d):
        return (x[0].bitcast(d), x[1], x[2])

    def bank(b, lo=0, hi=C):
        return v("ps", 512 * b + lo, 512 * b + hi)

    def op(q, f, outs, ins, sem=None, loose=False, val=16, adds=False):
        ins = [x for x in ins if isinstance(x, tuple)]
        w = [k for x in outs for k in x[1]]
        r = [k for x in ins for k in x[1]] + [k for x in outs + ins for k in x[2]]
        banks = {b for n, m in r + w if n == "ps" for b in range(8) if m >> (512 * b) & ((1 << 512) - 1)}
        ops.append({"q": q, "f": f, "r": r, "w": w, "sem": sem, "loose": loose, "val": val, "banks": banks, "sum": adds,
                    "names": {n for n, m in r + w}})

    def a_(x):
        return x[0] if isinstance(x, tuple) else x

    def ts(out, in0, s1, op0, s2=None, op1=None):
        if op1 is None:
            op("V", lambda: V.tensor_scalar(out[0], in0[0], a_(s1), None, op0), [out], [in0, s1])
        else:
            op("V", lambda: V.tensor_scalar(out[0], in0[0], a_(s1), a_(s2), op0, op1), [out], [in0, s1, s2])

    def tt(out, in0, in1, o):
        op("V", lambda: V.tensor_tensor(out[0], in0[0], in1[0], o), [out], [in0, in1])

    def cp(out, in_):
        op("V", lambda: V.tensor_copy(out[0], in_[0]), [out], [in_])

    def scan(out, d0, d1, init, op0, op1):
        op("V", lambda: V.tensor_tensor_scan(out[0], d0[0], d1[0], a_(init), op0, op1), [out], [d0, d1, init])

    def ms(out, x):
        op("V", lambda: V.memset(out[0], x), [out], [])

    def qz(codes, scales, tile):
        op("V", lambda: V.quantize_mx(codes[0], scales[0], tile[0]), [codes, scales], [tile])

    def act(out, in_, func, bias=0.0, scale=1.0, acc=None):
        if acc is None:
            op("S", lambda: S.activation(out[0], in_[0], func, bias=a_(bias), scale=scale), [out], [in_, bias])
        else:
            op("S", lambda: S.activation(out[0], in_[0], func, bias=a_(bias), scale=scale, accum_out=acc[0]), [out, acc], [in_, bias])

    def acp(out, in_):
        op("S", lambda: S.activation(out[0], in_[0], AF.Copy), [out], [in_])

    def times(e, out, in_, x):
        if e == "V":
            ts(out, in_, x, A.mult)
        else:
            op("S", lambda: S.activation(out[0], in_[0], AF.Copy, scale=x), [out], [in_])

    def mm(b, left, lo, right, r0, r1, start=True, stop=True):
        out, a = bank(b, 0, r1 - r0), [v(n, lo, lo + 128) for n in left] + [v(n, r0, r1) for n in right]
        op("P", lambda: g.tensor.matmul_mx(out[0], a[0][0], a[1][0], a[2][0], a[3][0], start, stop), [out], a, adds=not (start and stop))

    def iota(out, pattern, base, cm, real=False):
        if real:
            op("G", lambda: g.iota(out[0], pattern, base, cm, allow_small_or_imprecise_dtypes=True), [out], [])
        else:
            op("G", lambda: g.iota(out[0], pattern, base, cm), [out], [])

    def keep(out, in_, pattern, base, cm, how):
        op("G", lambda: g.affine_select(out[0], in_[0], pattern, how, 0.0, base, cm), [out], [in_])

    sent = [0]

    def send(peer, out, in_, sem):
        rid, pid, _se = topo.addr(peer)
        sent[0] += len(topo.engines(core, peer))
        op("G", lambda: g.remote_dma(out[0], in_[0], T.sem[sem], T.sem.sent, pid, rid, topo.mask(core, peer)), [], [in_], loose=True)

    def load(q, out, src, sem, after=()):
        e = g.sync if q == "Y" else S
        op(q, lambda: e.dma_start(out[0], src), [out], list(after), sem=sem)

    stores = {"sto": 0, "sty": 0}

    def store(q, sem, out, in_, r):
        stores[sem] += 16
        e = g.sync if q == "Y" else S
        op(q, lambda: e.dma_start(out, in_).then_inc(T.sem[sem], 16), [], [r], loose=True)

    load("S", v("ub"), T.u[:], "lu")
    load("Y", v("tt0", 0, 4 * H), T.x[:, 0:4 * H], "lxA")
    load("Y", v("tt0", 4 * H), T.x[:, 4 * H:4 * C], "lxB")

    iota(v("i16"), [[1, 16]], 128, -1)
    iota(v("ipm"), [[0, Q]], 0, 1)
    iota(v("iou"), [[1, 2], [16, 8]], 0, 0)
    iota(v("i23"), [[-16, Q]], H - 15, 0)
    ms(v("one"), 1.0)
    keep(v("gb"), v("one", 0, 512), [[16, 8], [0, 64]], 15, -1, A.is_ge)
    keep(v("gs"), v("gb"), [[-16, 8], [0, 64]], 0, 1, A.is_ge)
    keep(v("eb", 0, 514), v("one"), [[1, 514]], -2, -4, A.is_equal)
    ms(v("fl", 4 * AT[5], 4 * AT[7]), 0.0)
    ts(v("r16"), v("i16"), 15, A.bitwise_and)
    ts(v("rpm"), v("ipm"), 15, A.bitwise_and)
    ms(v("n16", 0, 1), -FAR)
    for lo, hi, x in ((0, M, 1.0), (M, C, 0.0), (C, C + M, 1.0)):
        times("S", v("tab", lo, hi), v("one", 0, hi - lo), x)
    ts(v("dm16"), v("r16"), 0, A.is_equal)
    cp(v("pm"), v("rpm"))
    cp(v("ou"), v("iou"))
    ts(v("m16"), v("dm16"), 2 * FAR, A.mult, -FAR, A.add)
    ts(v("n16", 1), v("dm16", 1), -2 * FAR, A.mult, FAR, A.add)
    ts(v("kp16"), v("r16"), 0, A.not_equal)
    ts(v("l16"), v("r16"), 15.0, A.is_equal, -LOCK, A.mult)
    ts(v("e16"), v("dm16"), BIG, A.mult)
    acp(v("am"), by(v("m16"), v("pm")))
    acp(v("km"), by(v("n16"), v("pm")))
    tt(v("ca"), v("rpm"), v("i23"), A.add)
    ms(v("acc"), 0.0)
    tt(v("a16"), v("e16"), v("l16"), A.add)
    ts(v("inv", 1, 2), v("dm16", 0, 1), LOCK, A.mult, H - BIG, A.add)
    ms(v("fl", 4 * AT[9]), 0.0)
    qz(v("qc", AT[5], AT[7]), v("sc", AT[5], AT[7]), v("fl", 4 * AT[5], 4 * AT[7]))
    for a in (3, 4, 7, 8):
        ms(v("fl", 4 * (AT[a + 1] - 48), 4 * AT[a + 1]), 0.0)
    qz(v("qu"), v("su"), v("ub"))
    qz(v("qc", AT[9]), v("sc", AT[9]), v("fl", 4 * AT[9]))
    ts(v("cb"), v("ca"), -1.0, A.mult, v("a16", 15, 16), A.add)
    ts(v("t16"), v("r16"), 1.0, A.is_equal, BIG, A.mult)
    tt(v("x23"), v("rpm"), v("i23"), A.subtract)
    ts(v("inv", 3, 4), v("dm16", 0, 1), LOCK, A.mult, -BIG, A.add)
    for c in (0, 8):
        cp(raw(v("qp", 16 * c, 16 * c + 128), dt.uint32), by(v("qu"), v("ou", c, c + 8), True))
        acp(v("sp", 16 * c, 16 * c + 128), by(v("su"), v("ou", c, c + 8)))
    tt(v("c16"), v("t16"), v("kp16"), A.max)
    ts(v("x24"), v("x23"), float(H - 15), A.add)
    ts(v("x25"), v("x23"), float(H - 15 - L), A.add)
    acp(v("kp"), by(v("kp16"), v("pm")))
    acp(v("ad"), by(v("a16"), v("pm")))

    def unit(b):
        at = 528 * (b % 2) + 2 - b // 2 * 2
        qz(v("qe", 128 * b, 128 * (b + 1)), v("se", 128 * b, 128 * (b + 1)), v("eb", at, at + 512))

    def slot(m, n, step=4, first=0):
        a = [m in rows for rows in QUADS].index(True)
        at = 4 * AT[a] + QUADS[a].index(m)
        return v("fl", at + first, at + 4 * n, step)

    def ends(name, rows, w=1):
        step = rows[1] - rows[0] if len(rows) > 1 else 1
        return v(name, w * rows[0] + w - 1, w * rows[-1] + w, w * step)

    def score(m):
        return v("hold", 16 * m + 15, 16 * m + 16)

    up, sums, gone = ("qp", "sp"), ("qc", "sc"), v("st", 1, 2)

    def scale(b):
        return 64.0 if "tA%d" % b in LAYER else 1.0

    def layer(w, t):
        lo = H if "B" in w else 0
        hi = lo + H
        if w[:2] == "qf":
            qz(v("qf", lo, hi), v("sf", lo, hi), v("ft", 4 * lo, 4 * hi))
            return
        if w[0] == "w":
            for b in range(4):
                mm(b if lo else 4 + b, ("qw", "sw"), 128 * b, ("qf", "sf"), lo, hi)
            return
        b = int(w[2])
        part, big = v("ft", 4 * lo + b, 4 * hi, 4), v("f64", C * b + lo, C * b + hi)
        new = v("win%d" % t, 2 * C * b + lo, 2 * C * b + hi)
        picked = by(v("win%d" % (t - 1), 2 * C * b, 2 * C * (b + 1)), v("off", lo // 16, hi // 16))
        if w[0] == "g":
            times(w[3], part, picked, 1.0 / scale(b))
        elif w[0] == "i":
            times("S", v("rs", C * b + lo, C * b + hi), bank(b if lo else 4 + b, 0, H), 0.015625)
        elif w[0] == "k":
            tt(v("tt%d" % t, 4 * lo + b, 4 * hi, 4), picked, v("rs", C * b + lo, C * b + hi), A.add)
        elif w[0] == "f":
            times(w[3], big, part, 64.0)
        elif w[0] == "t":
            tt(new, bank(b if lo else 4 + b, 0, H), big, A.add)
        else:
            times(w[3], v("tt%d" % t, 4 * lo + b, 4 * hi, 4), new, 0.015625)

    def leave(w):
        qt, sq = "qt%d" % R, "sq%d" % R
        if w == "hrow":
            acp(v("hrow"), by(v("htab"), v("off")))
            store("S", "sty", T.ot[:], T.hrow[0:128:16, :], v("hrow"))
            return
        lo = H if w in ("yB", "yb") else 0
        hi = lo + H
        if w in ("ya", "yb"):
            cp(v("ys", lo, hi), bank(lo // H + 4, 0, H))
            store("Y", "sto", T.y[:, lo:hi], T.ys[:, lo:hi], v("ys", lo, hi))
            return
        store("Y", "sto", T.oc[:, 4 * lo:4 * hi], T[qt][:, lo:hi].bitcast(dt.uint8), v(qt, lo, hi))
        mm(lo // H + 4, ("qv", "sv"), 0, (qt, sq), lo, hi)
        if lo:
            for k in range(4):
                store("S", "sty", T.osc[4 * k:4 * k + 4, :], T[sq][32 * k:32 * k + 4, :], v(sq))

    def count(w, t):
        peer = T.cores[rank ^ STEP[t]]
        state, rk = ("qt%d" % t, "sq%d" % t), "rk%d" % t
        half = w[-1]
        rows = list(range(*PART.get(half, PART["A"])))
        lo, hi = 16 * rows[0], 16 * rows[-1] + 16
        land = v("lA%d" % t) if half == "A" else v("lB%d" % t, rows[0] % K, rows[-1] % K + 1)
        scores = bank(0 if lo else 4, 0, H)
        if w[:4] == "send":
            send(peer, raw(v("lq%d" % t, lo, hi), dt.uint8), raw(v(state[0], lo, hi), dt.uint8), "ac%d" % t)
            if not lo:
                return
            ne = len(topo.engines(peer, core))
            lq, ls = v("lq%d" % t), v("ls%d" % t)
            send(peer, ls, v(state[1]), "ac%d" % t)
            op(None, None, [lq, ls], [], sem="ac%d" % t, val=3 * ne)
            for h in "ABUL":
                if "r" + h in LAYER + COUNT:
                    op(None, None, [v("l%s%d" % ("AB"[h != "A"], t), PART[h][0] % K, (PART[h][1] - 1) % K + 1)], [],
                       sem="a%s%d" % (h, t), val=ne)
            if t == 0:
                keep(v("eb", 528, 528 + 514), v("one"), [[1, 514]], -3, -4, A.is_equal)
                iota(v("val"), [[1, C]], 0, 0, real=True)
            if t == 1:
                iota(v("htab"), [[0, 2], [1, C]], 0, 0, real=True)
        elif w == "pA":
            mm(4, up, 0, state, 0, H)
            mm(5, up, 0, state, 0, H)
            if t == 0:
                qz(v("qg"), v("sg"), v("gs"))
        elif w == "pF":
            mm(0, up, 0, state, H, C)
            mm(1, up, 0, state, H, C)
            mm(2, up, 128, state, 0, C)
        elif w[:3] == "row":
            acp(v("row", lo, hi), bank(1 if lo else 5, 0, H))
        elif w[:2] == "mk":
            tt(v("mk", lo, hi), scores, v("am", lo, hi), A.min)
        elif w[:2] == "hd":
            scan(v("hold", lo, hi), v("km", lo, hi), v("mk", lo, hi), 0.0, A.min, A.max)
        elif w[:3] == "own":
            tt(slot(lo // 16, H), scores, v("hold", lo, hi), A.is_le)
        elif w[:2] == "cr":
            scan(v("cr", lo, hi), v("kp", lo, hi), slot(lo // 16, H), 0.0, A.mult, A.add)
        elif w == "n1":
            act(v("cf"), bank(2), AF.Sign)
        elif w == "n2":
            act(v("cf"), v("cf"), AF.Relu, acc=v("st", 0, 1))
        elif w == "n3":
            ts(gone, v("st", 0, 1), float(M), A.min)
        elif w == "lo":
            if t == 0:
                ms(v("b0"), 1.0)
                acp(v("ae"), by(v("a16"), v("pm")))
                ts(v("inv", 0, 1), v("dm16", 15, 16), 1.0 - 1.0 / BIG, A.mult, 1.0 / BIG, A.add)
                ts(v("inv", 2, 3), v("dm16", 15, 16), 1.0 - BIG, A.mult, BIG, A.add)
                ms(v("b0", 0, 4 * Q, 4), 0.0)
            ts(v("lo"), v(rk), gone, A.is_lt)
            ts(v("hi"), v(rk), gone, A.subtract, float(L), A.is_ge)
            ts(v("b1", 2, 4 * Q, 4), v(rk), -1.0, A.mult, -1.0, A.add)
            cp(v("b1", 3, 4 * Q, 4), v(rk))
            ts(v("st", 2, 3), gone, v("inv", 2, 3), A.mult)
        elif w == "out":
            tt(v("b0", 3, 4 * Q, 4), v("lo"), v("hi"), A.add)
        elif w == "w1":
            ts(v("v1"), v("x24"), gone, A.is_lt, float(C), A.mult)
            ts(v("v2"), v("x25"), gone, A.is_ge, float(C), A.mult)
        elif w == "w2":
            tt(v("v3"), v("v1"), v("v2"), A.add)
        elif w == "w3":
            ts(v("ae", 15, C, 16), v("v3"), v("a16", 15, 16), A.add)
        elif w[0] == "j":
            cp(by(v("npa"), land), v("nk", lo, hi))
        elif w == "side":
            for b in range(4 if t == 0 else 0):
                unit(b)
            if t == 1:
                qz(v("qv"), v("sv"), v("vb"))
        elif w[:2] == "cj":
            tt(ends("cj", rows), ends("cb", rows), ends("cr", rows, 16), A.subtract)
        elif w[0] in "xu":
            for run in runs([m for m in rows if ("s%d" % m in COUNT + LAYER) == (w[0] == "u")]):
                tt(ends("ad", run, 16), ends("cj", run), ends("acc", run) if w[0] == "x" else ends("zv", run, W), A.subtract)
        elif w[0] in "ev":
            for run in runs([m for m in rows if ("s%d" % (m + K) in COUNT + LAYER) == (w[0] == "v")]):
                far = [m + K for m in run]
                tt(ends("cj", run), ends("cj", run), ends("acc", far) if w[0] == "e" else ends("zv", far, W), A.subtract)
        elif w[0] == "d":
            scan(v("cd", lo, hi), bank({"A": 6, "L": 7}.get(half, 3), lo % H, lo % H + hi - lo), v("ad", lo, hi), 0.0, A.max, A.add)
        elif w[0] == "r":
            ts(ends(rk, rows), ends("cd", rows, 16), v("inv", 1, 2), A.add)
            send(peer, land, ends(rk, rows), "a%s%d" % (half, t))
        elif w[0] == "z":
            ts(ends("z16", rows), ends(rk, rows), gone, A.subtract, float(M), A.add)
        elif w[:2] == "nk":
            (cp if w[2] == "V" else acp)(v("nk", lo, hi), by(v("tab"), ends("z16", rows)))
        elif w[0] == "q":
            a0, a1 = int(w[1], 16), int(w[2], 16)
            qz(v("qc", AT[a0], AT[a1]), v("sc", AT[a0], AT[a1]), v("fl", 4 * AT[a0], 4 * AT[a1]))
            same = [x for x in LAYER + COUNT if x[0] == "q" and x[1].isdigit() and (x[1] > "6") == (a0 > 6)]
            if a0 > 6 and "rU" in LAYER + COUNT:
                for a in range(a0, min(a1, 9)):
                    mm(3, ("qg", "sg"), 0, sums, AT[a], AT[a + 1], a == 7, a == 8)
                for a in range(a0, min(a1, 10)):
                    mm(7, ("qg", "sg"), 0, sums, AT[a], AT[a] + 128, a == 7, a == 9)
                return
            for a in range(a0, a1):
                mm(3 if a0 > 6 else 6, ("qg", "sg"), 0, sums, AT[a], AT[a] + max(128, WIDE[a]),
                   w == same[0] and a == a0, w == same[-1] and a == a1 - 1)
        else:
            m = int(w[1:])
            n, upper = (16 * (m % K), m >= K) if m < Q else (H, False)
            mine = score(m if m < Q else m - K)
            row = v("row", H * upper, H * upper + n) if "row" + "AB"[upper] in LAYER + COUNT else None
            if w[0] == "c":
                ts(slot(m, n), row or bank(0 if upper else 4, 0, n), mine, A.is_lt)
            elif w[0] == "s":
                scan(v("zv", W * (m + 1) - n // 2, W * (m + 1)), slot(m, n, 8), slot(m, n, 8, 4), 0.0, A.add, A.add)
            elif w[0] == "h":
                act(v("fs", H * m, H * m + n), slot(m, n), AF.Relu, acc=v("acc", m, m + 1))
            elif w[0] == "a":
                act(v("fs", H * m, H * m + n), row or bank(1 if upper else 5, 0, n), AF.Sign, bias=mine, scale=-1.0)
            else:
                act(slot(m, n), v("fs", H * m, H * m + n), AF.Relu, acc=v("acc", m, m + 1))

    def children(t):
        win, rk, la, lb = "win%d" % t, v("rk%d" % t), v("lA%d" % t), v("lB%d" % t)

        def planes(b0, b1):
            for b in range(b0, b1):
                if t == 0 or scale(b) == 1.0:
                    times("S", v(win, 2 * C * b, 2 * C * b + C), v("tt%d" % t, b, 4 * C, 4), scale(b))

        if t == 0:
            acp(v("cm"), by(v("c16"), v("pm")))
            load("Y", raw(v("qw"), dt.uint8), T.wc[:], "lwc", [v("b0")])
            load("Y", v("sw"), T.ws[:], "lws")
        for b in range(4):
            mm(4 + b, ("qe", "se"), 128 * b, ("lq%d" % t, "ls%d" % t), 0, C)
        planes(0, 2)
        count("jL" if "rU" in LAYER + COUNT else "jB", t)
        scan(v("tc"), v("npa"), v("npa"), 0.0, A.add, A.max)
        cp(v("tx", 0, H), by(v("tc"), la))
        acp(v("tx", H), by(v("tc"), lb))
        planes(2, 4)
        for b in range(4):
            times("S", v(win, 2 * C * b + C, 2 * C * (b + 1)), bank(4 + b), scale(b))

        def step(w):
            lo = H if w[1] == "B" else 0
            b = lo // 4
            if w[0] == "d":
                scan(v("td", lo, lo + H), v("cm", lo, lo + H), v("tx", lo, lo + H), 0.0, A.mult, A.max)
            elif w[0] == "j":
                ts(v("b1", b, b + 4 * K, 4), v("td", lo + 15, lo + H, 16), v("inv", 0, 1), A.mult)
                ts(v("b1", b + 1, b + 4 * K, 4), v("td", lo + 15, lo + H, 16), v("st", 2, 3), A.is_gt, float(L), A.mult)
            elif w[0] == "o":
                scan(v("bo", b, b + 4 * K), v("b0", b, b + 4 * K), v("b1", b, b + 4 * K), 0.0, A.mult, A.add)
            elif w[0] == "p":
                cp(v("pl", lo // 16, lo // 16 + K), v("bo", b + 3, b + 4 * K, 4))
            else:
                cp(by(v("idx"), v("pl")), v("val"))

        for w in PLACE:
            step(w)
        for lo in (0, H):
            scan(v("idd", lo, lo + H), v("idx", lo, lo + H), v("ae", lo, lo + H), 0.0, A.max, A.add)
        for lo in (0, H):
            ts(v("off", lo // 16, lo // 16 + K), v("idd", lo + 15, lo + H, 16), v("inv", 3, 4), A.add)
        if t == 0:
            load("Y", v("vb"), T.v[:], "lv", [v("off")])

    for t in range(R + 1):
        order = LAYER + COUNT if t < R else LAST
        for w in order:
            if w in ("qA", "qB"):
                lo = H if w == "qB" else 0
                qz(v("qt%d" % t, lo, lo + H), v("sq%d" % t, lo, lo + H), v("tt%d" % t, 4 * lo, 4 * (lo + H)))
            elif w[0] == "y" or w == "hrow":
                if t == R:
                    leave(w)
            elif w[:2] == "qf" or w in ("wA", "wB") or (w[0] in "gftlik" and w[1] in "AB" and len(w) > 2):
                if t > 0:
                    layer(w, t)
            elif t < R:
                count(w, t)
        if t < R:
            children(t)
    schedule(g, T, ops)
    g.sync.wait_ge(T.sem.sto, stores["sto"])
    S.wait_ge(T.sem.sty, stores["sty"])
    g.wait_ge(T.sem.sent, sent[0])
